import numpy as np
import ml_dtypes


def mxq(x, axis, fmt="e4m3"):
    dtype, down = {"e4m3": (ml_dtypes.float8_e4m3fn, 7), "e5m2": (ml_dtypes.float8_e5m2, 14)}[fmt]
    v = np.moveaxis(np.asarray(x, np.float32).astype(ml_dtypes.bfloat16).astype(np.float64), axis, -1)
    blocks = v.reshape(v.shape[:-1] + (-1, 32))
    amax = np.abs(blocks).max(-1, keepdims=True)
    byte = np.maximum(np.where(amax > 0, np.frexp(amax)[1] - 1 + 127, 0) - down, 1)
    scale = np.exp2(byte - 127.0)
    codes = (blocks / scale).astype(np.float32).astype(dtype).astype(np.float64)
    return np.moveaxis((codes * scale).reshape(v.shape), -1, axis)


WIDE = False


def mx_kscale(k):
    if not WIDE:
        return np.ones(k)
    levels = np.array([10, -10, 5, -5, 0])
    if k % 512:
        return np.exp2(np.random.permutation(np.resize(levels, k // 32))).repeat(32)
    a = np.empty((k // 512, 16))
    for p in range(k // 512):
        a[p, :8] = np.random.permutation(np.resize(levels, 8))
        for g in range(8):
            far = levels[np.abs(levels - a[p, g]) >= 10]
            a[p, g + 8] = far[np.random.randint(len(far))]
    return np.exp2(a.ravel()).repeat(32)


BF16 = ml_dtypes.bfloat16


def bf(x):
    return np.asarray(x, np.float32).astype(BF16)


def f64(x):
    return np.asarray(x).astype(np.float64)


E2M1 = np.array([0.0, 0.5, 1.0, 1.5, 2.0, 3.0, 4.0, 6.0, -0.0, -0.5, -1.0, -1.5, -2.0, -3.0, -4.0, -6.0])


def pack_weight(w, fmt):
    k, n = w.shape
    w = f64(bf(w)).reshape(k // 32, 32, n)
    amax = np.abs(w).max(1)
    if fmt == "e4m3":
        byte = np.frexp(amax)[1] - 1 + 127 - 7
    else:
        mant, ex = np.frexp(amax / 6.0)
        byte = np.where(mant > 0.5, ex, ex - 1) + 127
    byte = np.clip(np.where(amax > 0, byte, 1), 1, 254)
    scaled = (w * np.exp2(127.0 - byte)[:, None, :]).reshape(k, n).astype(np.float32)
    by_word = np.ascontiguousarray(scaled.reshape(k // 512, 128, 4, n).transpose(0, 1, 3, 2))
    if fmt == "e4m3":
        words = by_word.astype(ml_dtypes.float8_e4m3fn).view(np.uint8)
    else:
        c = by_word.astype(ml_dtypes.float4_e2m1fn).view(np.uint8) & 0xF
        words = c[..., 0::2] | (c[..., 1::2] << 4)
    return np.ascontiguousarray(words), np.ascontiguousarray(byte.astype(np.uint8).reshape(k // 512, 16, n))


def unpack_weight(words, scales, fmt):
    g, p, n, _ = words.shape
    if fmt == "e4m3":
        vals = np.ascontiguousarray(words).view(ml_dtypes.float8_e4m3fn).astype(np.float64)
    else:
        nib = np.empty((g, p, n, 4), np.uint8)
        nib[..., 0::2] = words & 0xF
        nib[..., 1::2] = words >> 4
        vals = E2M1[nib]
    vals = vals * np.repeat(np.exp2(scales.astype(np.float64) - 127.0), 8, axis=1)[..., None]
    return vals.transpose(0, 1, 3, 2).reshape(g * 512, n)
def pack4(w):
    words, scales = pack_weight(w, "e2m1")
    return words.reshape(words.shape[0], 128, -1), scales


def unpack4(words, scales):
    return unpack_weight(words.reshape(words.shape[0], 128, -1, 2), scales, "e2m1")


R, F, T, D, C = 1024, 1024, 2048, 1536, 512


def draw0():
    s, u = mx_kscale(F), mx_kscale(D)
    v = mx_kscale(T)
    w_p = np.random.standard_normal((D, C)) / np.sqrt(D) / T ** 0.25 / u[:, None]
    w_p_words, w_p_scales = pack4(w_p)
    return {"w_f": bf(np.random.standard_normal((R, F)) / np.sqrt(F) / T ** 0.25 * s),
            "y_f": bf(np.random.standard_normal((F, T)) / s[:, None]),
            "z_p": bf(np.random.standard_normal((D, T)) * u[:, None] / v),
            "w_p_words": w_p_words,
            "w_p_scales": w_p_scales,
            "level": bf(0.3 * np.random.standard_normal(R) / T ** 0.25),
            "lam": bf(np.random.uniform(0.5, 1.5, T) * v),
            "rho": bf(1 + 0.1 * np.random.standard_normal(R))}


def core(w_f, y_f, z_p, w_p_words, w_p_scales, level, lam, rho):
    fut = mxq(f64(w_f), 1, "e4m3") @ mxq(f64(y_f), 0, "e4m3")
    fut = (fut + f64(level)[:, None]) * f64(lam)
    past = mxq(f64(z_p), 0, "e4m3").T @ unpack4(w_p_words, w_p_scales)
    h = mxq(fut, 1, "e4m3") @ mxq(past, 0, "e4m3")
    return h * f64(rho)[:, None]


def e4m3fn_bytes(y):
    return np.clip(np.asarray(y, np.float64), -448.0, 448.0).astype(np.float32).astype(ml_dtypes.float8_e4m3fn).view(np.uint8)


def e4m3fn_values(b):
    return np.asarray(b, np.uint8).view(ml_dtypes.float8_e4m3fn).astype(np.float64)


def setup_inputs():
    d = draw0()
    x0 = np.asarray(d['y_f']).astype(np.float64)
    s = (np.max(np.abs(x0), axis=(1,), keepdims=True) / 448.0).astype(np.float32)
    out = {}
    for k, v in d.items():
        if k == 'y_f':
            out['y_f_bytes'] = e4m3fn_bytes(x0 / s.astype(np.float64))
            out['y_f_scale'] = s
        else:
            out[k] = v
    return out


def reference(w_f, y_f_bytes, y_f_scale, z_p, w_p_words, w_p_scales, level, lam, rho):
    return core(w_f, e4m3fn_values(y_f_bytes) * y_f_scale.astype(np.float64), z_p, w_p_words, w_p_scales, level, lam, rho)

@@ -1,0 +1,631 @@
+from contextlib import ExitStack
+
+import concourse.mybir as mybir
+from concourse.masks import make_identity
+
+R, F, T, D, C = 1024, 1024, 2048, 1536, 512
+FLOPS = 2 * (R * F * T + T * D * C + R * T * C)
+
+F32 = mybir.dt.float32
+BF16 = mybir.dt.bfloat16
+U32 = mybir.dt.uint32
+I32 = mybir.dt.int32
+U8 = mybir.dt.uint8
+FP8 = mybir.dt.float8_e4m3fn
+FP8X4 = mybir.dt.float8_e4m3fn_x4
+FP4X4 = mybir.dt.float4_e2m1fn_x4
+ADD = mybir.AluOpType.add
+MULT = mybir.AluOpType.mult
+COPY = mybir.ActivationFunctionType.Copy
+
+P = 128
+GROUPS = T // 512
+FP = F // 512
+DP = D // 512
+RT = R // P
+OPEN = 4
+
+
+def tile_weighted_hankel_subspace_s11_kernel(
+    tc, w_f, y_f_bytes, y_f_scale, z_p, w_p_words, w_p_scales, level, lam, rho, out
+):
+    nc = tc.nc
+    with ExitStack() as ctx:
+        keep = ctx.enter_context(tc.tile_pool(name="keep", bufs=1))
+        work = ctx.enter_context(tc.tile_pool(name="work", bufs=2))
+        psum = ctx.enter_context(tc.psum_pool(name="psum", bufs=1))
+
+        ident = keep.tile([P, P], F32, name="ident")
+        make_identity(nc, ident[:])
+
+        y_scale = keep.tile([P, FP, 4], F32, name="y_scale")
+        lev16 = keep.tile([P, RT], BF16, name="lev16")
+        rho16 = keep.tile([P, RT], BF16, name="rho16")
+        lev = keep.tile([P, RT], F32, name="lev")
+        rhos = keep.tile([P, RT], F32, name="rhos")
+        lam_raw = keep.tile([P, T], BF16, name="lam_raw")
+        lam_ord = keep.tile([P, T], BF16, name="lam_ord")
+        wf = keep.tile([P, RT, F], BF16, name="wf", align_bytes=64)
+        wi = keep.tile([P, FP, R, 4], BF16, name="wi", align_bytes=64)
+        wcode = keep.tile([P, FP, R], U32, name="wcode", align_bytes=64)
+        wscale = keep.tile([P, FP, R], U8, name="wscale", align_bytes=64)
+        pw = keep.tile([P, DP, 2 * C], U8, name="pw", align_bytes=64)
+        pws = keep.tile([P, DP, C], U8, name="pws", align_bytes=64)
+        acode = keep.tile([P, GROUPS, R], U32, name="acode", align_bytes=64)
+        ascale = keep.tile([P, GROUPS, R], U8, name="ascale", align_bytes=64)
+        bcode = keep.tile([P, GROUPS, C], U32, name="bcode", align_bytes=64)
+        bscale = keep.tile([P, GROUPS, C], U8, name="bscale", align_bytes=64)
+
+        y_view = y_f_bytes.rearrange("(g p t) n -> g p t n", g=FP, p=P, t=4)
+        z_view = z_p.rearrange("(g p t) n -> g p t n", g=DP, p=P, t=4)
+        w_view = w_f.rearrange("(p c) f -> p c f", c=RT)
+        out_view = out.rearrange("(p c) n -> p c n", c=RT)
+
+        tiles = {}
+
+        def load_y(g, f):
+            if f == 0:
+                tiles["yb", g] = work.tile([P, FP, 4, 512], U8, name="yb", align_bytes=64)
+            nc.sync.dma_start(out=tiles["yb", g][:, f, :, :], in_=y_view[f][:, :, 512 * g : 512 * g + 512])
+
+        def load_z(g, d):
+            zr = work.tile([P, 4, 512], BF16, name="zr", bufs=8, align_bytes=64)
+            nc.sync.dma_start(out=zr[:], in_=z_view[d][:, :, 512 * g : 512 * g + 512])
+            tiles["zr", g, d] = zr
+
+        def load_w(c0, n):
+            nc.sync.dma_start(out=wf[:, c0 : c0 + n, :], in_=w_view[:, c0 : c0 + n, :])
+
+        def widen(g, f, t, eng):
+            if t == 0:
+                tiles["yw", g, f] = work.tile([P, 4, 512], BF16, name="yw", bufs=3, align_bytes=64)
+            src = tiles["yb", g][:, f, t, :].bitcast(FP8)
+            dst = tiles["yw", g, f][:, t, :]
+            s = y_scale[:, f, t : t + 1]
+            if eng == "S":
+                nc.scalar.activation(out=dst, in_=src, func=COPY, scale=s)
+            else:
+                nc.vector.tensor_scalar(out=dst, in0=src, scalar1=s, scalar2=None, op0=MULT)
+
+        def ilv_y(g, f, u, eng):
+            if u == 0:
+                tiles["yi", g, f] = work.tile([P, 512, 4], BF16, name="yi", bufs=3, align_bytes=64)
+            dst = tiles["yi", g, f][:, 256 * u : 256 * u + 256, :].rearrange("p (q e) t -> p q e t", e=2)
+            src = tiles["yw", g, f][:].rearrange("p t (q u e) -> p u q e t", u=2, e=2)[:, u]
+            if eng == "S":
+                nc.scalar.copy(out=dst, in_=src)
+            else:
+                nc.vector.tensor_copy(out=dst, in_=src)
+
+        def quant_y(g, f):
+            if f == 0:
+                tiles["yc", g] = work.tile([P, FP, 512], U32, name="yc", align_bytes=64)
+                tiles["ys", g] = work.tile([P, FP, 512], U8, name="ys", align_bytes=64)
+            nc.vector.quantize_mx(
+                out=tiles["yc", g][:, f, :].bitcast(FP8X4),
+                scales=tiles["ys", g][:, f, :],
+                in_=tiles["yi", g, f][:].rearrange("p n t -> p (n t)"),
+            )
+
+        def ilv_z(g, d, h, eng):
+            if h == 0:
+                tiles["zi", g, d] = work.tile([P, 4, 128, 4], BF16, name="zi", bufs=4, align_bytes=64)
+            dst = tiles["zi", g, d][:, 2 * h : 2 * h + 2]
+            src = tiles["zr", g, d][:].rearrange("p j (m s) -> p s m j", s=4)[:, 2 * h : 2 * h + 2]
+            if eng == "S":
+                nc.scalar.copy(out=dst, in_=src)
+            else:
+                nc.vector.tensor_copy(out=dst, in_=src)
+
+        def quant_z(g, d):
+            if d == 0:
+                tiles["zc", g] = work.tile([P, DP, 512], U32, name="zc", align_bytes=64)
+                tiles["zs", g] = work.tile([P, DP, 512], U8, name="zs", align_bytes=64)
+            nc.vector.quantize_mx(
+                out=tiles["zc", g][:, d, :].bitcast(FP8X4),
+                scales=tiles["zs", g][:, d, :],
+                in_=tiles["zi", g, d][:].rearrange("p s m j -> p (s m j)"),
+            )
+
+        def w_transpose(c):
+            tag = W_TAGS[c]
+            wt = psum.tile([P, FP, 2, P], F32, name=tag, bufs=PS[tag])
+            words = wf[:, c, :].bitcast(F32)
+            for f in range(FP):
+                for u in range(2):
+                    nc.tensor.transpose(wt[:, f, u, :], words[:, 256 * f + u : 256 * (f + 1) : 2], ident[:])
+            tiles["wt", c] = wt
+
+        def w_copy(c, eng):
+            dst = wi[:].rearrange("p f r j -> p (f r j)").bitcast(F32)
+            dst = dst.rearrange("p (f r u) -> p f r u", f=FP, u=2)[:, :, P * c : P * c + P, :]
+            src = tiles["wt", c][:].rearrange("p f u r -> p f r u")
+            if eng == "S":
+                nc.scalar.copy(out=dst, in_=src)
+            else:
+                nc.vector.tensor_copy(out=dst, in_=src)
+
+        def w_quant(f, r0, n):
+            nc.vector.quantize_mx(
+                out=wcode[:, f, r0 : r0 + n].bitcast(FP8X4),
+                scales=wscale[:, f, r0 : r0 + n],
+                in_=wi[:, f, r0 : r0 + n, :].rearrange("p r j -> p (r j)"),
+            )
+
+        PS = {"fut": 2, "past": 1, "tr": 1}
+        W_TAGS = ["fut", "tr", "past", "fut", "tr", "past", "fut", "tr"]
+        H_TAGS = ["h0", "h1", "h2", "h3", "fut", "past", "fut", "tr"]
+
+        def past(g, cc):
+            pp = psum.tile([P, 4, 128], F32, name="past", bufs=PS["past"])
+            for s in range(4):
+                for d in range(DP):
+                    nc.tensor.matmul_mx(
+                        out=pp[:, s, :],
+                        lhsT=tiles["zc", g][:, d, 128 * s : 128 * s + 128].bitcast(FP8X4),
+                        lhsT_scale=tiles["zs", g][:, d, 128 * s : 128 * s + 128],
+                        rhs=pw[:, d, 256 * cc : 256 * cc + 256].bitcast(FP4X4),
+                        rhs_scale=pws[:, d, 128 * cc : 128 * cc + 128],
+                        start=(d == 0),
+                        stop=(d == DP - 1),
+                    )
+            tiles["pp", g, cc] = pp
+
+        def past_copy(g, cc, eng):
+            if cc == 0:
+                tiles["pi", g] = work.tile([P, 512, 4], BF16, name="pi", align_bytes=64)
+            dst = tiles["pi", g][:, 128 * cc : 128 * cc + 128, :]
+            src = tiles["pp", g, cc][:].rearrange("p s n -> p n s")
+            if eng == "S":
+                nc.scalar.copy(out=dst, in_=src)
+            else:
+                nc.vector.tensor_copy(out=dst, in_=src)
+
+        def quant_past(g):
+            nc.vector.quantize_mx(
+                out=bcode[:, g, :].bitcast(FP8X4),
+                scales=bscale[:, g, :],
+                in_=tiles["pi", g][:].rearrange("p n s -> p (n s)"),
+            )
+
+        def fut(g, c):
+            fp = psum.tile([P, 512], F32, name="fut", bufs=PS["fut"])
+            for f in range(FP):
+                nc.tensor.matmul_mx(
+                    out=fp[:],
+                    lhsT=wcode[:, f, P * c : P * c + P].bitcast(FP8X4),
+                    lhsT_scale=wscale[:, f, P * c : P * c + P],
+                    rhs=tiles["yc", g][:, f, :].bitcast(FP8X4),
+                    rhs_scale=tiles["ys", g][:, f, :],
+                    start=(f == 0),
+                    stop=(f == FP - 1),
+                )
+            tiles["fp", g, c] = fp
+
+        def a_op(g, c):
+            at = work.tile([P, 512], BF16, name="at", bufs=5, align_bytes=64)
+            nc.vector.scalar_tensor_tensor(
+                out=at[:],
+                in0=tiles["fp", g, c][:],
+                scalar=lev[:, c : c + 1],
+                in1=lam_ord[:, 512 * g : 512 * g + 512],
+                op0=ADD,
+                op1=MULT,
+            )
+            tiles["at", g, c] = at
+
+        def tr(q):
+            g, c0 = q // 4, 2 * (q % 4)
+            tp = psum.tile([P, 2, 2, P], F32, name="tr", bufs=PS["tr"])
+            for k in range(2):
+                words = tiles["at", g, c0 + k][:].bitcast(F32)
+                for u in range(2):
+                    nc.tensor.transpose(tp[:, k, u, :], words[:, P * u : P * u + P], ident[:])
+            tiles["tp", q] = tp
+
+        def tr_copy(q, eng):
+            g, c0 = q // 4, 2 * (q % 4)
+            if c0 == 0:
+                tiles["ai", g] = work.tile([P, R, 4], BF16, name="ai", align_bytes=64)
+            dst = tiles["ai", g][:].rearrange("p r j -> p (r j)").bitcast(F32)
+            dst = dst.rearrange("p (c r u) -> p c r u", r=P, u=2)[:, c0 : c0 + 2]
+            src = tiles["tp", q][:].rearrange("p c u r -> p c r u")
+            if eng == "S":
+                nc.scalar.copy(out=dst, in_=src)
+            else:
+                nc.vector.tensor_copy(out=dst, in_=src)
+
+        def quant_a(q, n):
+            g, r0 = q // 4, 256 * (q % 4)
+            nc.vector.quantize_mx(
+                out=acode[:, g, r0 : r0 + 256 * n].bitcast(FP8X4),
+                scales=ascale[:, g, r0 : r0 + 256 * n],
+                in_=tiles["ai", g][:, r0 : r0 + 256 * n, :].rearrange("p r j -> p (r j)"),
+            )
+
+        def h_pass(c, g):
+            tag = H_TAGS[c]
+            if g == 0:
+                tiles["h", c] = psum.tile([P, C], F32, name=tag, bufs=PS.get(tag, 1))
+            nc.tensor.matmul_mx(
+                out=tiles["h", c][:],
+                lhsT=acode[:, g, P * c : P * c + P].bitcast(FP8X4),
+                lhsT_scale=ascale[:, g, P * c : P * c + P],
+                rhs=bcode[:, g, :].bitcast(FP8X4),
+                rhs_scale=bscale[:, g, :],
+                start=(g == 0),
+                stop=(g == GROUPS - 1),
+            )
+
+        def h_out(c, eng):
+            if c == 0:
+                tiles["ho"] = keep.tile([P, RT, C], F32, name="wf", align_bytes=64)
+            ho = tiles["ho"][:, c, :]
+            if eng == "S":
+                nc.scalar.activation(out=ho, in_=tiles["h", c][:], func=COPY, scale=rhos[:, c : c + 1])
+            else:
+                nc.vector.tensor_scalar(
+                    out=ho, in0=tiles["h", c][:], scalar1=rhos[:, c : c + 1], scalar2=None, op0=MULT
+                )
+            nc.sync.dma_start(out=out_view[:, c, :], in_=ho)
+
+        def load_lam(g0, g1):
+            nc.sync.dma_start(
+                out=lam_raw[:, 512 * g0 : 512 * g1], in_=lam[512 * g0 : 512 * g1].partition_broadcast(P)
+            )
+
+        def order_lam(g0, g1):
+            nc.vector.tensor_copy(
+                out=lam_ord[:, 512 * g0 : 512 * g1].bitcast(F32).rearrange("p (g u q) -> p g u q", g=g1 - g0, u=2),
+                in_=lam_raw[:, 512 * g0 : 512 * g1].bitcast(F32).rearrange("p (g q u) -> p g u q", g=g1 - g0, u=2),
+            )
+
+
+        def small_loads():
+            nc.scalar.dma_start(out=y_scale[:], in_=y_f_scale.rearrange("(g p t) o -> p g (t o)", g=FP, p=P, t=4))
+            nc.scalar.dma_start(out=lev16[:], in_=level.rearrange("(p c) -> p c", c=RT))
+            nc.scalar.dma_start(out=rho16[:], in_=rho.rearrange("(p c) -> p c", c=RT))
+
+        def load_pw():
+            nc.sync.dma_start(out=pw[:], in_=w_p_words.rearrange("d p n -> p d n"))
+
+        def clear_pws():
+            nc.vector.memset(pws[:].rearrange("p d n -> p (d n)").bitcast(I32), 0)
+
+        def load_pws():
+            for q in range(4):
+                nc.sync.dma_start(
+                    out=pws[32 * q : 32 * q + 4, :, :].bitcast(I32),
+                    in_=w_p_scales[:, 4 * q : 4 * q + 4, :].rearrange("d q n -> q d n").bitcast(I32),
+                )
+
+        def widen_small():
+            nc.vector.tensor_copy(out=lev[:], in_=lev16[:])
+            nc.vector.tensor_copy(out=rhos[:], in_=rho16[:])
+
+        with tc.manual_schedule():
+            load_y(0, 0)
+            small_loads()
+            widen(0, 0, 0, "S")
+            load_y(0, 1)
+            widen(0, 0, 1, "V")
+            load_w(0, 2)
+            widen(0, 0, 3, "V")
+            widen(0, 0, 2, "V")
+            load_y(1, 0)
+            ilv_y(0, 0, 0, "V")
+            ilv_y(0, 0, 1, "V")
+            widen(0, 1, 0, "V")
+            widen(0, 1, 3, "S")
+            load_z(0, 0)
+            load_lam(0, 1)
+            w_transpose(0)
+            clear_pws()
+            widen(0, 1, 1, "S")
+            load_w(2, 2)
+            widen(0, 1, 2, "S")
+            load_y(1, 1)
+            ilv_y(0, 1, 0, "V")
+            quant_y(0, 0)
+            ilv_z(0, 0, 0, "V")
+            widen(1, 0, 0, "S")
+            load_w(4, 2)
+            w_transpose(1)
+            widen(1, 0, 2, "V")
+            load_w(6, 2)
+            ilv_y(0, 1, 1, "S")
+            widen(1, 0, 3, "S")
+            widen(1, 0, 1, "V")
+            w_transpose(3)
+            order_lam(0, 1)
+            load_z(0, 1)
+            ilv_y(1, 0, 0, "V")
+            w_transpose(2)
+            widen_small()
+            w_copy(1, "S")
+            load_z(0, 2)
+            ilv_y(1, 0, 1, "V")
+            w_copy(0, "S")
+            ilv_z(0, 0, 1, "S")
+            quant_y(0, 1)
+            quant_y(1, 0)
+            w_transpose(4)
+            load_y(2, 0)
+            w_copy(2, "S")
+            load_z(1, 0)
+            quant_z(0, 0)
+            widen(1, 1, 0, "V")
+            w_copy(3, "S")
+            w_quant(0, 0, 512)
+            load_pw()
+            w_copy(4, "S")
+            load_pws()
+            w_transpose(7)
+            widen(1, 1, 2, "S")
+            load_z(1, 1)
+            widen(1, 1, 1, "V")
+            w_transpose(6)
+            w_copy(7, "S")
+            widen(1, 1, 3, "S")
+            w_quant(1, 0, 512)
+            fut(0, 0)
+            w_copy(6, "S")
+            w_transpose(5)
+            ilv_z(0, 1, 0, "V")
+            fut(0, 1)
+            w_copy(5, "S")
+            ilv_y(1, 1, 0, "S")
+            ilv_z(0, 2, 0, "S")
+            a_op(0, 0)
+            fut(0, 2)
+            ilv_z(0, 1, 1, "S")
+            ilv_y(1, 1, 1, "V")
+            ilv_z(0, 2, 1, "V")
+            ilv_z(1, 0, 0, "S")
+            a_op(0, 1)
+            widen(2, 0, 0, "S")
+            w_quant(0, 512, 512)
+            tr(0)
+            fut(0, 3)
+            w_quant(1, 512, 512)
+            a_op(0, 2)
+            ilv_z(1, 0, 1, "V")
+            load_y(2, 1)
+            tr_copy(0, "S")
+            quant_z(0, 1)
+            fut(0, 4)
+            a_op(0, 3)
+            quant_z(0, 2)
+            load_lam(1, 4)
+            widen(2, 0, 3, "S")
+            quant_z(1, 0)
+            fut(0, 5)
+            quant_y(1, 1)
+            a_op(0, 4)
+            a_op(0, 5)
+            widen(2, 0, 2, "V")
+            past(0, 0)
+            past_copy(0, 0, "S")
+            tr(1)
+            tr_copy(1, "S")
+            fut(0, 6)
+            widen(2, 1, 0, "V")
+            a_op(0, 6)
+            load_z(1, 2)
+            ilv_z(1, 1, 0, "S")
+            widen(2, 0, 1, "V")
+            past(0, 1)
+            order_lam(1, 4)
+            past_copy(0, 1, "S")
+            fut(0, 7)
+            tr(2)
+            a_op(0, 7)
+            fut(1, 0)
+            widen(2, 1, 1, "V")
+            ilv_z(1, 1, 1, "S")
+            tr_copy(2, "S")
+            past(0, 2)
+            fut(1, 1)
+            ilv_z(1, 2, 0, "V")
+            a_op(1, 0)
+            ilv_y(2, 0, 0, "V")
+            widen(2, 1, 2, "S")
+            fut(1, 2)
+            tr(3)
+            a_op(1, 1)
+            fut(1, 3)
+            load_z(2, 0)
+            load_z(2, 1)
+            past_copy(0, 2, "S")
+            ilv_z(1, 2, 1, "S")
+            tr_copy(3, "S")
+            quant_a(0, 2)
+            a_op(1, 2)
+            quant_z(1, 1)
+            a_op(1, 3)
+            ilv_y(2, 0, 1, "V")
+            past(0, 3)
+            fut(1, 4)
+            load_y(3, 0)
+            ilv_z(2, 0, 0, "S")
+            tr(4)
+            quant_z(1, 2)
+            past_copy(0, 3, "S")
+            widen(2, 1, 3, "S")
+            fut(1, 5)
+            widen(3, 0, 0, "S")
+            past(1, 0)
+            quant_past(0)
+            tr_copy(4, "S")
+            past_copy(1, 0, "S")
+            h_pass(1, 0)
+            ilv_y(2, 1, 0, "S")
+            h_pass(2, 0)
+            past(1, 1)
+            a_op(1, 4)
+            past_copy(1, 1, "S")
+            load_z(2, 2)
+            h_pass(3, 0)
+            fut(1, 6)
+            widen(3, 0, 1, "V")
+            quant_y(2, 0)
+            ilv_y(2, 1, 1, "V")
+            ilv_z(2, 1, 0, "S")
+            past(1, 2)
+            tr(5)
+            past_copy(1, 2, "S")
+            ilv_z(2, 0, 1, "V")
+            a_op(1, 5)
+            quant_y(2, 1)
+            a_op(1, 6)
+            load_y(3, 1)
+            widen(3, 1, 0, "V")
+            fut(1, 7)
+            fut(2, 0)
+            quant_z(2, 0)
+            a_op(1, 7)
+            past(1, 3)
+            ilv_z(2, 1, 1, "S")
+            ilv_z(2, 2, 0, "V")
+            widen(3, 0, 2, "V")
+            tr_copy(5, "S")
+            quant_z(2, 1)
+            ilv_z(2, 2, 1, "S")
+            past_copy(1, 3, "S")
+            a_op(2, 0)
+            tr(6)
+            load_z(3, 0)
+            fut(2, 1)
+            fut(2, 2)
+            quant_z(2, 2)
+            widen(3, 0, 3, "S")
+            past(2, 0)
+            a_op(2, 1)
+            load_z(3, 1)
+            a_op(2, 2)
+            tr_copy(6, "S")
+            fut(2, 3)
+            widen(3, 1, 2, "S")
+            tr(7)
+            fut(2, 4)
+            ilv_y(3, 0, 0, "V")
+            a_op(2, 3)
+            past_copy(2, 0, "S")
+            past(2, 1)
+            widen(3, 1, 1, "V")
+            fut(2, 5)
+            a_op(2, 4)
+            ilv_z(3, 0, 0, "S")
+            tr_copy(7, "S")
+            widen(3, 1, 3, "S")
+            quant_past(1)
+            h_pass(0, 0)
+            tr(8)
+            quant_a(2, 2)
+            load_z(3, 2)
+            quant_a(4, 2)
+            fut(2, 6)
+            past_copy(2, 1, "S")
+            tr_copy(8, "S")
+            ilv_y(3, 0, 1, "V")
+            past(2, 2)
+            ilv_z(3, 1, 0, "S")
+            a_op(2, 5)
+            quant_y(3, 0)
+            past_copy(2, 2, "S")
+            ilv_y(3, 1, 0, "S")
+            ilv_z(3, 0, 1, "V")
+            h_pass(1, 1)
+            ilv_y(3, 1, 1, "V")
+            a_op(2, 6)
+            h_pass(3, 1)
+            tr(9)
+            quant_y(3, 1)
+            fut(2, 7)
+            past(2, 3)
+            tr_copy(9, "S")
+            a_op(2, 7)
+            h_pass(2, 1)
+            tr(10)
+            ilv_z(3, 2, 0, "V")
+            fut(3, 0)
+            ilv_z(3, 1, 1, "S")
+            tr_copy(10, "S")
+            fut(3, 1)
+            a_op(3, 0)
+            a_op(3, 1)
+            h_pass(0, 1)
+            tr(11)
+            ilv_z(3, 2, 1, "S")
+            tr_copy(11, "S")
+            quant_z(3, 0)
+            fut(3, 2)
+            quant_z(3, 1)
+            quant_z(3, 2)
+            past_copy(2, 3, "S")
+            fut(3, 3)
+            tr(12)
+            a_op(3, 2)
+            a_op(3, 3)
+            past(3, 0)
+            past_copy(3, 0, "V")
+            fut(3, 4)
+            quant_a(6, 2)
+            a_op(3, 4)
+            tr_copy(12, "V")
+            fut(3, 5)
+            past(3, 1)
+            a_op(3, 5)
+            past_copy(3, 1, "S")
+            fut(3, 6)
+            tr(13)
+            past(3, 2)
+            fut(3, 7)
+            quant_a(8, 2)
+            past_copy(3, 2, "S")
+            quant_past(2)
+            h_pass(1, 2)
+            a_op(3, 6)
+            h_pass(4, 0)
+            tr_copy(13, "S")
+            a_op(3, 7)
+            past(3, 3)
+            tr(14)
+            h_pass(6, 0)
+            h_pass(3, 2)
+            past_copy(3, 3, "S")
+            quant_a(10, 2)
+            quant_a(12, 2)
+            tr_copy(14, "S")
+            quant_past(3)
+            h_pass(0, 2)
+            h_pass(2, 2)
+            tr(15)
+            h_pass(0, 3)
+            h_out(0, "S")
+            h_pass(1, 3)
+            tr_copy(15, "S")
+            h_pass(4, 1)
+            h_pass(4, 2)
+            h_pass(2, 3)
+            h_pass(3, 3)
+            h_pass(7, 0)
+            h_pass(7, 1)
+            h_pass(7, 2)
+            h_out(1, "V")
+            quant_a(14, 2)
+            h_pass(7, 3)
+            h_pass(4, 3)
+            h_out(2, "S")
+            h_pass(5, 0)
+            h_pass(6, 1)
+            h_pass(6, 2)
+            h_pass(6, 3)
+            h_out(3, "S")
+            h_pass(5, 1)
+            h_pass(5, 2)
+            h_pass(5, 3)
+            h_out(7, "V")
+            h_out(4, "S")
+            h_out(6, "V")
+            h_out(5, "V")

@@ -36,14 +36,17 @@ def tile_weighted_hankel_subspace_s11_kernel(
         psum = ctx.enter_context(tc.psum_pool(name="psum", bufs=1))
 
         ident = keep.tile([P, P], F32, name="ident")
-        make_identity(nc, ident[:])
 
+        make_identity(nc, ident[:])
         y_scale = keep.tile([P, FP, 4], F32, name="y_scale")
         lev16 = keep.tile([P, RT], BF16, name="lev16")
         rho16 = keep.tile([P, RT], BF16, name="rho16")
         lev = keep.tile([P, RT], F32, name="lev")
         rhos = keep.tile([P, RT], F32, name="rhos")
-        lam_raw = keep.tile([P, T], BF16, name="lam_raw")
+        lam_row = keep.tile([P, T], BF16, name="lam_row")
+        ones = keep.tile([P, P], BF16, name="ones")
+        nc.gpsimd.memset(lam_row[:], 0.0)
+        nc.gpsimd.memset(ones[:], 1.0)
         lam_ord = keep.tile([P, T], BF16, name="lam_ord")
         wf = keep.tile([P, RT, F], BF16, name="wf", align_bytes=64)
         wi = keep.tile([P, FP, R, 4], BF16, name="wi", align_bytes=64)
@@ -90,8 +93,8 @@ def tile_weighted_hankel_subspace_s11_kernel(
         def ilv_y(g, f, u, eng):
             if u == 0:
                 tiles["yi", g, f] = work.tile([P, 512, 4], BF16, name="yi", bufs=3, align_bytes=64)
-            dst = tiles["yi", g, f][:, 256 * u : 256 * u + 256, :].rearrange("p (q e) t -> p q e t", e=2)
-            src = tiles["yw", g, f][:].rearrange("p t (q u e) -> p u q e t", u=2, e=2)[:, u]
+            dst = tiles["yi", g, f][:, 256 * u : 256 * u + 256, :].rearrange("p (q e) t -> p q t e", e=2)
+            src = tiles["yw", g, f][:].rearrange("p t (q u e) -> p u q t e", u=2, e=2)[:, u]
             if eng == "S":
                 nc.scalar.copy(out=dst, in_=src)
             else:
@@ -110,8 +113,8 @@ def tile_weighted_hankel_subspace_s11_kernel(
         def ilv_z(g, d, h, eng):
             if h == 0:
                 tiles["zi", g, d] = work.tile([P, 4, 128, 4], BF16, name="zi", bufs=4, align_bytes=64)
-            dst = tiles["zi", g, d][:, 2 * h : 2 * h + 2]
-            src = tiles["zr", g, d][:].rearrange("p j (m s) -> p s m j", s=4)[:, 2 * h : 2 * h + 2]
+            dst = tiles["zi", g, d][:].rearrange("p s m j -> p m j s")[:, 64 * h : 64 * h + 64]
+            src = tiles["zr", g, d][:].rearrange("p j (m s) -> p m j s", s=4)[:, 64 * h : 64 * h + 64]
             if eng == "S":
                 nc.scalar.copy(out=dst, in_=src)
             else:
@@ -269,16 +272,24 @@ def tile_weighted_hankel_subspace_s11_kernel(
                 )
             nc.sync.dma_start(out=out_view[:, c, :], in_=ho)
 
-        def load_lam(g0, g1):
-            nc.sync.dma_start(
-                out=lam_raw[:, 512 * g0 : 512 * g1], in_=lam[512 * g0 : 512 * g1].partition_broadcast(P)
-            )
+        def load_lam():
+            nc.sync.dma_start(out=lam_row[0:1, :], in_=lam.rearrange("(o n) -> o n", o=1))
 
-        def order_lam(g0, g1):
-            nc.vector.tensor_copy(
-                out=lam_ord[:, 512 * g0 : 512 * g1].bitcast(F32).rearrange("p (g u q) -> p g u q", g=g1 - g0, u=2),
-                in_=lam_raw[:, 512 * g0 : 512 * g1].bitcast(F32).rearrange("p (g q u) -> p g u q", g=g1 - g0, u=2),
-            )
+        def spread_lam(i):
+            lp = psum.tile([P, 2, 512], BF16, name="h%d" % i)
+            for k in range(2):
+                g = 2 * i + k
+                nc.tensor.matmul(out=lp[:, k, :], lhsT=ones[:], rhs=lam_row[:, 512 * g : 512 * g + 512], start=True, stop=True)
+            tiles["lp", i] = lp
+
+        def order_lam(i, k, eng):
+            g = 2 * i + k
+            dst = lam_ord[:, 512 * g : 512 * g + 512].rearrange("p (u q e) -> p u q e", u=2, e=2)
+            src = tiles["lp", i][:, k, :].rearrange("p (q u e) -> p u q e", u=2, e=2)
+            if eng == "S":
+                nc.scalar.copy(out=dst, in_=src)
+            else:
+                nc.vector.tensor_copy(out=dst, in_=src)
 
 
         def small_loads():
@@ -306,326 +317,329 @@ def tile_weighted_hankel_subspace_s11_kernel(
         with tc.manual_schedule():
             load_y(0, 0)
             small_loads()
-            widen(0, 0, 0, "S")
             load_y(0, 1)
-            widen(0, 0, 1, "V")
-            load_w(0, 2)
-            widen(0, 0, 3, "V")
+            widen(0, 0, 0, "S")
             widen(0, 0, 2, "V")
-            load_y(1, 0)
-            ilv_y(0, 0, 0, "V")
-            ilv_y(0, 0, 1, "V")
-            widen(0, 1, 0, "V")
-            widen(0, 1, 3, "S")
+            widen(0, 0, 1, "V")
             load_z(0, 0)
-            load_lam(0, 1)
-            w_transpose(0)
-            clear_pws()
-            widen(0, 1, 1, "S")
-            load_w(2, 2)
-            widen(0, 1, 2, "S")
-            load_y(1, 1)
-            ilv_y(0, 1, 0, "V")
-            quant_y(0, 0)
-            ilv_z(0, 0, 0, "V")
-            widen(1, 0, 0, "S")
-            load_w(4, 2)
-            w_transpose(1)
-            widen(1, 0, 2, "V")
-            load_w(6, 2)
-            ilv_y(0, 1, 1, "S")
-            widen(1, 0, 3, "S")
-            widen(1, 0, 1, "V")
-            w_transpose(3)
-            order_lam(0, 1)
             load_z(0, 1)
-            ilv_y(1, 0, 0, "V")
+            widen(0, 0, 3, "V")
+            ilv_y(0, 0, 0, "S")
+            widen(0, 1, 0, "V")
+            load_w(2, 2)
             w_transpose(2)
+            load_w(0, 2)
+            widen(0, 1, 3, "V")
+            ilv_y(0, 0, 1, "V")
+            ilv_z(0, 0, 0, "V")
             widen_small()
-            w_copy(1, "S")
-            load_z(0, 2)
-            ilv_y(1, 0, 1, "V")
-            w_copy(0, "S")
-            ilv_z(0, 0, 1, "S")
-            quant_y(0, 1)
-            quant_y(1, 0)
-            w_transpose(4)
-            load_y(2, 0)
+            widen(0, 1, 2, "S")
+            w_transpose(0)
+            widen(0, 1, 1, "S")
+            ilv_z(0, 1, 0, "S")
+            w_transpose(3)
             w_copy(2, "S")
-            load_z(1, 0)
-            quant_z(0, 0)
-            widen(1, 1, 0, "V")
+            quant_y(0, 0)
+            ilv_z(0, 0, 1, "V")
+            ilv_y(0, 1, 0, "V")
+            load_y(1, 0)
+            w_transpose(1)
+            ilv_z(0, 1, 1, "V")
+            load_lam()
+            w_copy(0, "S")
+            load_y(1, 1)
+            ilv_y(0, 1, 1, "V")
+            spread_lam(1)
+            load_w(4, 2)
+            load_z(0, 2)
             w_copy(3, "S")
-            w_quant(0, 0, 512)
-            load_pw()
-            w_copy(4, "S")
-            load_pws()
-            w_transpose(7)
-            widen(1, 1, 2, "S")
-            load_z(1, 1)
-            widen(1, 1, 1, "V")
-            w_transpose(6)
-            w_copy(7, "S")
-            widen(1, 1, 3, "S")
-            w_quant(1, 0, 512)
-            fut(0, 0)
-            w_copy(6, "S")
-            w_transpose(5)
-            ilv_z(0, 1, 0, "V")
-            fut(0, 1)
-            w_copy(5, "S")
-            ilv_y(1, 1, 0, "S")
-            ilv_z(0, 2, 0, "S")
-            a_op(0, 0)
-            fut(0, 2)
-            ilv_z(0, 1, 1, "S")
-            ilv_y(1, 1, 1, "V")
-            ilv_z(0, 2, 1, "V")
-            ilv_z(1, 0, 0, "S")
-            a_op(0, 1)
-            widen(2, 0, 0, "S")
-            w_quant(0, 512, 512)
-            tr(0)
-            fut(0, 3)
-            w_quant(1, 512, 512)
-            a_op(0, 2)
-            ilv_z(1, 0, 1, "V")
-            load_y(2, 1)
-            tr_copy(0, "S")
+            spread_lam(0)
+            quant_z(0, 0)
+            clear_pws()
             quant_z(0, 1)
+            quant_y(0, 1)
+            load_w(6, 2)
+            widen(1, 0, 0, "S")
+            widen(1, 0, 1, "V")
+            w_copy(1, "S")
+            widen(1, 0, 3, "S")
+            widen(1, 1, 0, "V")
+            w_quant(1, 0, 512)
+            w_transpose(4)
+            widen(1, 1, 1, "S")
+            w_transpose(5)
+            widen(1, 0, 2, "S")
+            w_copy(4, "S")
+            w_transpose(6)
+            load_y(2, 0)
+            w_transpose(7)
+            w_quant(0, 0, 512)
+            ilv_z(0, 2, 0, "S")
+            w_copy(5, "S")
+            load_pw()
+            load_z(1, 0)
+            fut(0, 0)
+            order_lam(0, 0, "V")
+            ilv_y(1, 0, 0, "V")
+            w_copy(6, "S")
+            w_copy(7, "S")
+            order_lam(0, 1, "S")
+            fut(0, 1)
+            widen(2, 0, 0, "S")
+            widen(1, 1, 2, "V")
+            widen(1, 1, 3, "V")
+            ilv_z(0, 2, 1, "V")
+            widen(2, 0, 3, "S")
+            order_lam(1, 0, "V")
+            quant_z(0, 2)
+            ilv_y(1, 1, 0, "V")
+            ilv_y(1, 0, 1, "S")
+            widen(2, 0, 1, "V")
+            load_y(2, 1)
+            a_op(0, 0)
+            a_op(0, 1)
+            load_pws()
+            fut(0, 2)
+            tr(0)
+            tr_copy(0, "S")
+            load_z(1, 1)
+            w_quant(0, 512, 512)
+            ilv_z(1, 0, 0, "S")
+            fut(0, 3)
+            a_op(0, 2)
+            load_z(1, 2)
+            w_quant(1, 512, 512)
             fut(0, 4)
             a_op(0, 3)
-            quant_z(0, 2)
-            load_lam(1, 4)
-            widen(2, 0, 3, "S")
-            quant_z(1, 0)
-            fut(0, 5)
-            quant_y(1, 1)
-            a_op(0, 4)
-            a_op(0, 5)
-            widen(2, 0, 2, "V")
-            past(0, 0)
-            past_copy(0, 0, "S")
-            tr(1)
-            tr_copy(1, "S")
-            fut(0, 6)
             widen(2, 1, 0, "V")
-            a_op(0, 6)
-            load_z(1, 2)
-            ilv_z(1, 1, 0, "S")
-            widen(2, 0, 1, "V")
-            past(0, 1)
-            order_lam(1, 4)
-            past_copy(0, 1, "S")
+            tr(1)
+            fut(0, 5)
+            a_op(0, 4)
+            fut(0, 6)
+            quant_y(1, 0)
+            past(0, 0)
+            ilv_y(1, 1, 1, "V")
+            a_op(0, 5)
             fut(0, 7)
-            tr(2)
+            widen(2, 0, 2, "S")
+            tr_copy(1, "S")
+            quant_a(0, 2)
+            a_op(0, 6)
+            widen(2, 1, 1, "S")
+            quant_y(1, 1)
             a_op(0, 7)
+            past_copy(0, 0, "S")
+            tr(2)
+            ilv_z(1, 0, 1, "V")
+            ilv_z(1, 1, 0, "S")
             fut(1, 0)
-            widen(2, 1, 1, "V")
-            ilv_z(1, 1, 1, "S")
-            tr_copy(2, "S")
-            past(0, 2)
-            fut(1, 1)
-            ilv_z(1, 2, 0, "V")
-            a_op(1, 0)
-            ilv_y(2, 0, 0, "V")
-            widen(2, 1, 2, "S")
-            fut(1, 2)
-            tr(3)
-            a_op(1, 1)
-            fut(1, 3)
             load_z(2, 0)
+            widen(2, 1, 3, "V")
+            tr_copy(2, "S")
+            ilv_z(1, 1, 1, "S")
+            past(0, 1)
+            a_op(1, 0)
+            past_copy(0, 1, "S")
+            load_y(3, 0)
+            fut(1, 1)
+            widen(2, 1, 2, "V")
+            a_op(1, 1)
+            tr(3)
+            ilv_z(1, 2, 0, "S")
+            quant_z(1, 0)
+            fut(1, 2)
+            past(0, 2)
+            a_op(1, 2)
+            fut(1, 3)
+            ilv_z(1, 2, 1, "V")
+            ilv_y(2, 0, 0, "V")
+            a_op(1, 3)
+            quant_z(1, 1)
+            tr_copy(3, "S")
+            tr(4)
+            fut(1, 4)
+            fut(1, 5)
+            a_op(1, 4)
             load_z(2, 1)
             past_copy(0, 2, "S")
-            ilv_z(1, 2, 1, "S")
-            tr_copy(3, "S")
-            quant_a(0, 2)
-            a_op(1, 2)
-            quant_z(1, 1)
-            a_op(1, 3)
-            ilv_y(2, 0, 1, "V")
-            past(0, 3)
-            fut(1, 4)
-            load_y(3, 0)
-            ilv_z(2, 0, 0, "S")
-            tr(4)
-            quant_z(1, 2)
-            past_copy(0, 3, "S")
-            widen(2, 1, 3, "S")
-            fut(1, 5)
-            widen(3, 0, 0, "S")
-            past(1, 0)
-            quant_past(0)
+            ilv_y(2, 0, 1, "S")
             tr_copy(4, "S")
-            past_copy(1, 0, "S")
-            h_pass(1, 0)
-            ilv_y(2, 1, 0, "S")
-            h_pass(2, 0)
-            past(1, 1)
-            a_op(1, 4)
-            past_copy(1, 1, "S")
-            load_z(2, 2)
-            h_pass(3, 0)
-            fut(1, 6)
-            widen(3, 0, 1, "V")
-            quant_y(2, 0)
+            ilv_y(2, 1, 0, "V")
+            quant_z(1, 2)
+            past(0, 3)
+            ilv_z(2, 0, 0, "S")
+            past_copy(0, 3, "S")
             ilv_y(2, 1, 1, "V")
-            ilv_z(2, 1, 0, "S")
-            past(1, 2)
-            tr(5)
-            past_copy(1, 2, "S")
-            ilv_z(2, 0, 1, "V")
             a_op(1, 5)
-            quant_y(2, 1)
-            a_op(1, 6)
-            load_y(3, 1)
-            widen(3, 1, 0, "V")
-            fut(1, 7)
-            fut(2, 0)
-            quant_z(2, 0)
-            a_op(1, 7)
-            past(1, 3)
-            ilv_z(2, 1, 1, "S")
-            ilv_z(2, 2, 0, "V")
-            widen(3, 0, 2, "V")
+            tr(5)
             tr_copy(5, "S")
-            quant_z(2, 1)
-            ilv_z(2, 2, 1, "S")
-            past_copy(1, 3, "S")
-            a_op(2, 0)
+            fut(1, 6)
+            ilv_z(2, 0, 1, "V")
+            load_y(3, 1)
+            past(1, 0)
+            widen(3, 0, 0, "S")
             tr(6)
-            load_z(3, 0)
-            fut(2, 1)
-            fut(2, 2)
-            quant_z(2, 2)
-            widen(3, 0, 3, "S")
-            past(2, 0)
-            a_op(2, 1)
-            load_z(3, 1)
-            a_op(2, 2)
+            quant_y(2, 0)
+            fut(1, 7)
+            order_lam(1, 1, "S")
+            load_z(2, 2)
+            past_copy(1, 0, "S")
+            ilv_z(2, 1, 0, "S")
+            a_op(1, 6)
+            past(1, 1)
+            quant_y(2, 1)
+            fut(2, 0)
+            quant_past(0)
+            h_pass(2, 0)
+            past_copy(1, 1, "S")
+            a_op(1, 7)
             tr_copy(6, "S")
-            fut(2, 3)
-            widen(3, 1, 2, "S")
+            ilv_z(2, 2, 0, "S")
+            a_op(2, 0)
+            h_pass(1, 0)
+            past(1, 2)
+            ilv_z(2, 2, 1, "V")
+            fut(2, 1)
+            past_copy(1, 2, "S")
+            load_z(3, 0)
+            quant_a(4, 2)
+            quant_a(2, 2)
+            widen(3, 0, 1, "V")
+            h_pass(3, 0)
+            h_pass(0, 0)
+            a_op(2, 1)
+            fut(2, 2)
             tr(7)
-            fut(2, 4)
-            ilv_y(3, 0, 0, "V")
+            quant_z(2, 0)
+            quant_z(2, 2)
+            a_op(2, 2)
+            fut(2, 3)
+            ilv_z(2, 1, 1, "S")
             a_op(2, 3)
+            quant_z(2, 1)
+            widen(3, 1, 0, "V")
+            widen(3, 1, 1, "S")
+            past(1, 3)
+            tr_copy(7, "S")
+            widen(3, 0, 3, "S")
+            fut(2, 4)
+            widen(3, 0, 2, "S")
+            past_copy(1, 3, "S")
+            tr(8)
+            tr_copy(8, "S")
+            a_op(2, 4)
+            fut(2, 5)
+            widen(3, 1, 3, "V")
+            widen(3, 1, 2, "V")
+            past(2, 0)
+            quant_past(1)
+            load_z(3, 1)
+            fut(2, 6)
+            tr(9)
+            a_op(2, 5)
+            ilv_y(3, 0, 0, "V")
+            ilv_y(3, 0, 1, "S")
+            fut(2, 7)
+            ilv_y(3, 1, 0, "V")
             past_copy(2, 0, "S")
             past(2, 1)
-            widen(3, 1, 1, "V")
-            fut(2, 5)
-            a_op(2, 4)
             ilv_z(3, 0, 0, "S")
-            tr_copy(7, "S")
-            widen(3, 1, 3, "S")
-            quant_past(1)
-            h_pass(0, 0)
-            tr(8)
-            quant_a(2, 2)
-            load_z(3, 2)
-            quant_a(4, 2)
-            fut(2, 6)
-            past_copy(2, 1, "S")
-            tr_copy(8, "S")
-            ilv_y(3, 0, 1, "V")
-            past(2, 2)
-            ilv_z(3, 1, 0, "S")
-            a_op(2, 5)
-            quant_y(3, 0)
-            past_copy(2, 2, "S")
-            ilv_y(3, 1, 0, "S")
-            ilv_z(3, 0, 1, "V")
-            h_pass(1, 1)
             ilv_y(3, 1, 1, "V")
-            a_op(2, 6)
-            h_pass(3, 1)
-            tr(9)
-            quant_y(3, 1)
-            fut(2, 7)
-            past(2, 3)
-            tr_copy(9, "S")
-            a_op(2, 7)
-            h_pass(2, 1)
-            tr(10)
-            ilv_z(3, 2, 0, "V")
-            fut(3, 0)
-            ilv_z(3, 1, 1, "S")
-            tr_copy(10, "S")
-            fut(3, 1)
-            a_op(3, 0)
-            a_op(3, 1)
             h_pass(0, 1)
-            tr(11)
-            ilv_z(3, 2, 1, "S")
-            tr_copy(11, "S")
-            quant_z(3, 0)
+            tr_copy(9, "S")
+            past_copy(2, 1, "S")
+            quant_y(3, 0)
+            a_op(2, 6)
+            quant_y(3, 1)
+            a_op(2, 7)
+            h_pass(3, 1)
+            tr(10)
+            ilv_z(3, 0, 1, "V")
+            past(2, 2)
+            fut(3, 0)
+            a_op(3, 0)
+            ilv_z(3, 1, 0, "S")
+            fut(3, 1)
+            tr_copy(10, "S")
+            h_pass(1, 1)
+            past_copy(2, 2, "S")
             fut(3, 2)
+            ilv_z(3, 1, 1, "S")
+            load_z(3, 2)
+            tr(11)
+            ilv_z(3, 2, 0, "S")
+            a_op(3, 1)
+            fut(3, 3)
+            quant_z(3, 0)
+            past(2, 3)
+            tr_copy(11, "S")
+            a_op(3, 2)
+            ilv_z(3, 2, 1, "V")
+            a_op(3, 3)
             quant_z(3, 1)
             quant_z(3, 2)
-            past_copy(2, 3, "S")
-            fut(3, 3)
-            tr(12)
-            a_op(3, 2)
-            a_op(3, 3)
-            past(3, 0)
-            past_copy(3, 0, "V")
-            fut(3, 4)
             quant_a(6, 2)
-            a_op(3, 4)
-            tr_copy(12, "V")
+            fut(3, 4)
+            past_copy(2, 3, "S")
             fut(3, 5)
-            past(3, 1)
-            a_op(3, 5)
-            past_copy(3, 1, "S")
+            tr(12)
+            past(3, 0)
+            a_op(3, 4)
+            tr_copy(12, "S")
             fut(3, 6)
+            past_copy(3, 0, "S")
+            a_op(3, 5)
             tr(13)
-            past(3, 2)
-            fut(3, 7)
-            quant_a(8, 2)
-            past_copy(3, 2, "S")
-            quant_past(2)
-            h_pass(1, 2)
-            a_op(3, 6)
-            h_pass(4, 0)
             tr_copy(13, "S")
-            a_op(3, 7)
-            past(3, 3)
+            a_op(3, 6)
+            quant_past(2)
+            past(3, 1)
+            quant_a(8, 2)
             tr(14)
-            h_pass(6, 0)
-            h_pass(3, 2)
-            past_copy(3, 3, "S")
-            quant_a(10, 2)
-            quant_a(12, 2)
-            tr_copy(14, "S")
-            quant_past(3)
-            h_pass(0, 2)
-            h_pass(2, 2)
+            fut(3, 7)
+            past_copy(3, 1, "S")
+            past(3, 2)
+            tr_copy(14, "V")
+            a_op(3, 7)
             tr(15)
-            h_pass(0, 3)
-            h_out(0, "S")
-            h_pass(1, 3)
-            tr_copy(15, "S")
-            h_pass(4, 1)
-            h_pass(4, 2)
-            h_pass(2, 3)
-            h_pass(3, 3)
+            h_pass(4, 0)
+            past_copy(3, 2, "S")
+            past(3, 3)
+            h_pass(0, 2)
+            past_copy(3, 3, "S")
+            tr_copy(15, "V")
+            quant_a(12, 2)
+            h_pass(6, 0)
+            h_pass(6, 1)
             h_pass(7, 0)
             h_pass(7, 1)
-            h_pass(7, 2)
-            h_out(1, "V")
+            quant_a(10, 2)
+            h_pass(1, 2)
+            quant_past(3)
             quant_a(14, 2)
-            h_pass(7, 3)
-            h_pass(4, 3)
-            h_out(2, "S")
+            h_pass(0, 3)
             h_pass(5, 0)
-            h_pass(6, 1)
+            h_out(0, "V")
+            h_pass(1, 3)
             h_pass(6, 2)
+            h_out(1, "V")
             h_pass(6, 3)
-            h_out(3, "S")
+            h_out(6, "V")
+            h_pass(7, 2)
+            h_pass(7, 3)
             h_pass(5, 1)
             h_pass(5, 2)
             h_pass(5, 3)
+            h_pass(4, 1)
+            h_pass(4, 2)
+            h_pass(4, 3)
             h_out(7, "V")
-            h_out(4, "S")
-            h_out(6, "V")
-            h_out(5, "V")
+            h_pass(3, 2)
+            h_out(5, "S")
+            h_pass(3, 3)
+            h_out(4, "V")
+            h_pass(2, 1)
+            h_out(3, "S")
+            h_pass(2, 2)
+            h_pass(2, 3)
+            h_out(2, "V")

@@ -69,7 +69,11 @@ def tile_weighted_hankel_subspace_s11_kernel(
         def load_y(g, f):
             if f == 0:
                 tiles["yb", g] = work.tile([P, FP, 4, 512], U8, name="yb", align_bytes=64)
-            nc.sync.dma_start(out=tiles["yb", g][:, f, :, :], in_=y_view[f][:, :, 512 * g : 512 * g + 512])
+            step = 2 if (g, f) == (0, 0) else 4
+            for t in range(0, 4, step):
+                nc.sync.dma_start(
+                    out=tiles["yb", g][:, f, t : t + step, :], in_=y_view[f][:, t : t + step, 512 * g : 512 * g + 512]
+                )
 
         def load_z(g, d):
             zr = work.tile([P, 4, 512], BF16, name="zr", bufs=8, align_bytes=64)
@@ -155,9 +159,9 @@ def tile_weighted_hankel_subspace_s11_kernel(
                 in_=wi[:, f, r0 : r0 + n, :].rearrange("p r j -> p (r j)"),
             )
 
-        PS = {"fut": 2, "past": 1, "tr": 1}
-        W_TAGS = ["fut", "tr", "past", "fut", "tr", "past", "fut", "tr"]
-        H_TAGS = ["h0", "h1", "h2", "h3", "fut", "past", "fut", "tr"]
+        PS = {"fut": 2, "past": 2}
+        W_TAGS = ["fut", "past", "fut", "past", "fut", "past", "fut", "past"]
+        H_TAGS = ["h0", "h1", "h2", "h3", "fut", "past", "fut", "past"]
 
         def past(g, cc):
             pp = psum.tile([P, 4, 128], F32, name="past", bufs=PS["past"])
@@ -206,7 +210,7 @@ def tile_weighted_hankel_subspace_s11_kernel(
             tiles["fp", g, c] = fp
 
         def a_op(g, c):
-            at = work.tile([P, 512], BF16, name="at", bufs=5, align_bytes=64)
+            at = work.tile([P, 512], BF16, name="at", bufs=7, align_bytes=64)
             nc.vector.scalar_tensor_tensor(
                 out=at[:],
                 in0=tiles["fp", g, c][:],
@@ -218,13 +222,14 @@ def tile_weighted_hankel_subspace_s11_kernel(
             tiles["at", g, c] = at
 
         def tr(q):
-            g, c0 = q // 4, 2 * (q % 4)
-            tp = psum.tile([P, 2, 2, P], F32, name="tr", bufs=PS["tr"])
             for k in range(2):
-                words = tiles["at", g, c0 + k][:].bitcast(F32)
-                for u in range(2):
-                    nc.tensor.transpose(tp[:, k, u, :], words[:, P * u : P * u + P], ident[:])
-            tiles["tp", q] = tp
+                tp = psum.tile([P, 2, 2, P], F32, name="past", bufs=PS["past"])
+                for i in range(2):
+                    j = 4 * q + 2 * k + i
+                    words = tiles["at", j // RT, j % RT][:].bitcast(F32)
+                    for u in range(2):
+                        nc.tensor.transpose(tp[:, i, u, :], words[:, P * u : P * u + P], ident[:])
+                tiles["tp", 2 * q + k] = tp
 
         def tr_copy(q, eng):
             g, c0 = q // 4, 2 * (q % 4)
@@ -316,330 +321,326 @@ def tile_weighted_hankel_subspace_s11_kernel(
 
         with tc.manual_schedule():
             load_y(0, 0)
+            clear_pws()
             small_loads()
             load_y(0, 1)
-            widen(0, 0, 0, "S")
-            widen(0, 0, 2, "V")
-            widen(0, 0, 1, "V")
-            load_z(0, 0)
-            load_z(0, 1)
-            widen(0, 0, 3, "V")
-            ilv_y(0, 0, 0, "S")
-            widen(0, 1, 0, "V")
-            load_w(2, 2)
-            w_transpose(2)
-            load_w(0, 2)
-            widen(0, 1, 3, "V")
-            ilv_y(0, 0, 1, "V")
-            ilv_z(0, 0, 0, "V")
-            widen_small()
-            widen(0, 1, 2, "S")
-            w_transpose(0)
-            widen(0, 1, 1, "S")
-            ilv_z(0, 1, 0, "S")
-            w_transpose(3)
-            w_copy(2, "S")
-            quant_y(0, 0)
-            ilv_z(0, 0, 1, "V")
-            ilv_y(0, 1, 0, "V")
             load_y(1, 0)
-            w_transpose(1)
-            ilv_z(0, 1, 1, "V")
-            load_lam()
-            w_copy(0, "S")
-            load_y(1, 1)
-            ilv_y(0, 1, 1, "V")
-            spread_lam(1)
+            widen(0, 0, 0, "V")
+            load_w(0, 2)
+            widen(0, 0, 1, "S")
+            widen(0, 0, 3, "V")
+            widen(0, 0, 2, "V")
+            ilv_y(0, 0, 0, "V")
+            widen(0, 1, 0, "S")
+            load_z(0, 0)
+            load_w(2, 2)
+            widen(0, 1, 1, "S")
+            ilv_y(0, 0, 1, "V")
+            widen(0, 1, 2, "V")
             load_w(4, 2)
-            load_z(0, 2)
-            w_copy(3, "S")
-            spread_lam(0)
-            quant_z(0, 0)
-            clear_pws()
-            quant_z(0, 1)
-            quant_y(0, 1)
             load_w(6, 2)
+            widen(0, 1, 3, "S")
+            load_lam()
+            w_transpose(1)
+            load_y(1, 1)
+            w_transpose(0)
+            quant_y(0, 0)
+            load_z(0, 1)
             widen(1, 0, 0, "S")
-            widen(1, 0, 1, "V")
-            w_copy(1, "S")
-            widen(1, 0, 3, "S")
-            widen(1, 1, 0, "V")
-            w_quant(1, 0, 512)
-            w_transpose(4)
-            widen(1, 1, 1, "S")
-            w_transpose(5)
             widen(1, 0, 2, "S")
-            w_copy(4, "S")
-            w_transpose(6)
-            load_y(2, 0)
-            w_transpose(7)
-            w_quant(0, 0, 512)
-            ilv_z(0, 2, 0, "S")
-            w_copy(5, "S")
+            widen(1, 0, 3, "S")
+            load_z(0, 2)
+            w_transpose(2)
             load_pw()
-            load_z(1, 0)
-            fut(0, 0)
-            order_lam(0, 0, "V")
-            ilv_y(1, 0, 0, "V")
-            w_copy(6, "S")
-            w_copy(7, "S")
-            order_lam(0, 1, "S")
-            fut(0, 1)
-            widen(2, 0, 0, "S")
-            widen(1, 1, 2, "V")
-            widen(1, 1, 3, "V")
-            ilv_z(0, 2, 1, "V")
-            widen(2, 0, 3, "S")
-            order_lam(1, 0, "V")
-            quant_z(0, 2)
-            ilv_y(1, 1, 0, "V")
-            ilv_y(1, 0, 1, "S")
-            widen(2, 0, 1, "V")
-            load_y(2, 1)
-            a_op(0, 0)
-            a_op(0, 1)
+            ilv_y(0, 1, 0, "V")
+            w_transpose(3)
             load_pws()
-            fut(0, 2)
-            tr(0)
-            tr_copy(0, "S")
+            w_copy(0, "S")
+            load_y(2, 0)
+            load_z(1, 0)
             load_z(1, 1)
-            w_quant(0, 512, 512)
-            ilv_z(1, 0, 0, "S")
-            fut(0, 3)
-            a_op(0, 2)
+            ilv_y(0, 1, 1, "V")
+            widen(1, 0, 1, "S")
+            w_copy(1, "S")
+            ilv_y(1, 0, 0, "S")
+            w_copy(3, "S")
+            w_copy(2, "S")
             load_z(1, 2)
-            w_quant(1, 512, 512)
-            fut(0, 4)
+            widen_small()
+            ilv_z(0, 0, 0, "V")
+            ilv_z(0, 0, 1, "V")
+            quant_y(0, 1)
+            quant_z(0, 0)
+            w_transpose(5)
+            w_transpose(4)
+            w_copy(4, "S")
+            w_quant(1, 0, 256)
+            load_y(2, 1)
+            w_copy(5, "S")
+            w_transpose(7)
+            w_transpose(6)
+            w_copy(7, "S")
+            w_quant(0, 0, 256)
+            load_z(2, 0)
+            fut(0, 0)
+            load_z(2, 1)
+            ilv_y(1, 0, 1, "V")
+            w_quant(0, 256, 256)
+            spread_lam(0)
+            quant_y(1, 0)
+            w_copy(6, "S")
+            fut(0, 1)
+            w_quant(1, 256, 256)
+            w_quant(0, 512, 256)
+            w_quant(1, 512, 256)
+            widen(1, 1, 0, "V")
+            load_z(2, 2)
+            widen(1, 1, 1, "V")
+            w_quant(1, 768, 256)
+            widen(1, 1, 2, "S")
+            order_lam(0, 0, "S")
+            widen(1, 1, 3, "S")
+            w_quant(0, 768, 256)
+            a_op(0, 0)
+            ilv_z(0, 1, 0, "V")
+            fut(0, 2)
+            ilv_z(0, 1, 1, "S")
+            a_op(0, 1)
+            a_op(0, 2)
+            ilv_z(0, 2, 0, "S")
+            spread_lam(1)
+            fut(0, 3)
+            quant_z(0, 1)
+            ilv_z(0, 2, 1, "V")
             a_op(0, 3)
-            widen(2, 1, 0, "V")
-            tr(1)
+            fut(0, 4)
             fut(0, 5)
             a_op(0, 4)
+            load_y(3, 0)
             fut(0, 6)
-            quant_y(1, 0)
-            past(0, 0)
-            ilv_y(1, 1, 1, "V")
+            quant_z(0, 2)
+            ilv_y(1, 1, 0, "S")
             a_op(0, 5)
-            fut(0, 7)
-            widen(2, 0, 2, "S")
-            tr_copy(1, "S")
-            quant_a(0, 2)
-            a_op(0, 6)
-            widen(2, 1, 1, "S")
+            ilv_y(1, 1, 1, "S")
+            past(0, 0)
+            past(0, 1)
+            load_y(3, 1)
+            load_z(3, 0)
             quant_y(1, 1)
-            a_op(0, 7)
+            order_lam(0, 1, "S")
+            order_lam(1, 0, "S")
+            load_z(3, 1)
+            a_op(0, 6)
+            order_lam(1, 1, "S")
+            widen(2, 0, 0, "S")
+            widen(2, 0, 3, "V")
+            fut(0, 7)
             past_copy(0, 0, "S")
-            tr(2)
+            widen(2, 0, 1, "V")
+            past_copy(0, 1, "S")
+            tr(0)
+            widen(2, 0, 2, "V")
+            ilv_z(1, 0, 0, "S")
+            tr_copy(0, "S")
+            fut(1, 0)
+            ilv_y(2, 0, 0, "V")
+            past(0, 2)
+            tr_copy(1, "S")
+            past(0, 3)
+            ilv_y(2, 0, 1, "V")
             ilv_z(1, 0, 1, "V")
             ilv_z(1, 1, 0, "S")
-            fut(1, 0)
-            load_z(2, 0)
-            widen(2, 1, 3, "V")
-            tr_copy(2, "S")
-            ilv_z(1, 1, 1, "S")
-            past(0, 1)
-            a_op(1, 0)
-            past_copy(0, 1, "S")
-            load_y(3, 0)
+            quant_y(2, 0)
+            a_op(0, 7)
             fut(1, 1)
-            widen(2, 1, 2, "V")
-            a_op(1, 1)
-            tr(3)
-            ilv_z(1, 2, 0, "S")
             quant_z(1, 0)
-            fut(1, 2)
-            past(0, 2)
-            a_op(1, 2)
-            fut(1, 3)
-            ilv_z(1, 2, 1, "V")
-            ilv_y(2, 0, 0, "V")
-            a_op(1, 3)
+            past_copy(0, 2, "S")
+            ilv_z(1, 1, 1, "V")
+            past_copy(0, 3, "S")
+            a_op(1, 0)
+            tr(1)
             quant_z(1, 1)
+            fut(1, 2)
+            ilv_z(1, 2, 0, "V")
+            a_op(1, 1)
+            ilv_z(1, 2, 1, "S")
+            tr_copy(2, "S")
+            fut(1, 3)
             tr_copy(3, "S")
-            tr(4)
+            widen(2, 1, 0, "V")
+            quant_z(1, 2)
+            load_z(3, 2)
+            ilv_z(2, 0, 0, "S")
+            a_op(1, 2)
+            past(1, 0)
+            quant_past(0)
+            ilv_z(2, 0, 1, "S")
+            a_op(1, 3)
+            quant_a(0, 2)
+            past(1, 1)
             fut(1, 4)
             fut(1, 5)
+            past_copy(1, 0, "S")
+            widen(2, 1, 1, "V")
+            widen(2, 1, 2, "V")
+            h_pass(1, 0)
+            past_copy(1, 1, "S")
+            ilv_z(2, 1, 0, "S")
+            widen(2, 1, 3, "V")
             a_op(1, 4)
-            load_z(2, 1)
-            past_copy(0, 2, "S")
-            ilv_y(2, 0, 1, "S")
+            a_op(1, 5)
+            tr(2)
             tr_copy(4, "S")
             ilv_y(2, 1, 0, "V")
-            quant_z(1, 2)
-            past(0, 3)
-            ilv_z(2, 0, 0, "S")
-            past_copy(0, 3, "S")
-            ilv_y(2, 1, 1, "V")
-            a_op(1, 5)
-            tr(5)
-            tr_copy(5, "S")
             fut(1, 6)
-            ilv_z(2, 0, 1, "V")
-            load_y(3, 1)
-            past(1, 0)
-            widen(3, 0, 0, "S")
-            tr(6)
-            quant_y(2, 0)
-            fut(1, 7)
-            order_lam(1, 1, "S")
-            load_z(2, 2)
-            past_copy(1, 0, "S")
-            ilv_z(2, 1, 0, "S")
-            a_op(1, 6)
-            past(1, 1)
-            quant_y(2, 1)
-            fut(2, 0)
-            quant_past(0)
-            h_pass(2, 0)
-            past_copy(1, 1, "S")
-            a_op(1, 7)
-            tr_copy(6, "S")
-            ilv_z(2, 2, 0, "S")
-            a_op(2, 0)
-            h_pass(1, 0)
-            past(1, 2)
-            ilv_z(2, 2, 1, "V")
-            fut(2, 1)
-            past_copy(1, 2, "S")
-            load_z(3, 0)
-            quant_a(4, 2)
-            quant_a(2, 2)
-            widen(3, 0, 1, "V")
-            h_pass(3, 0)
-            h_pass(0, 0)
-            a_op(2, 1)
-            fut(2, 2)
-            tr(7)
             quant_z(2, 0)
-            quant_z(2, 2)
-            a_op(2, 2)
-            fut(2, 3)
-            ilv_z(2, 1, 1, "S")
-            a_op(2, 3)
-            quant_z(2, 1)
+            ilv_y(2, 1, 1, "V")
+            ilv_z(2, 2, 0, "S")
+            a_op(1, 6)
+            tr_copy(5, "S")
+            fut(1, 7)
+            h_pass(3, 0)
+            widen(3, 0, 0, "S")
+            past(1, 2)
+            quant_y(2, 1)
+            past_copy(1, 2, "S")
             widen(3, 1, 0, "V")
-            widen(3, 1, 1, "S")
+            h_pass(0, 0)
+            fut(2, 0)
+            a_op(1, 7)
+            widen(3, 1, 2, "V")
+            ilv_z(2, 2, 1, "V")
+            quant_a(4, 2)
             past(1, 3)
-            tr_copy(7, "S")
-            widen(3, 0, 3, "S")
-            fut(2, 4)
-            widen(3, 0, 2, "S")
+            ilv_z(2, 1, 1, "S")
+            h_pass(2, 0)
+            a_op(2, 0)
+            fut(2, 1)
             past_copy(1, 3, "S")
-            tr(8)
-            tr_copy(8, "S")
+            quant_z(2, 2)
+            a_op(2, 1)
+            tr(3)
+            ilv_z(3, 0, 0, "S")
+            quant_past(1)
+            quant_z(2, 1)
+            fut(2, 2)
+            fut(2, 3)
+            tr_copy(6, "S")
+            h_pass(2, 1)
+            ilv_z(3, 1, 0, "S")
+            a_op(2, 2)
+            quant_a(2, 2)
+            h_pass(0, 1)
+            past(2, 0)
+            widen(3, 0, 3, "V")
+            tr_copy(7, "S")
+            widen(3, 1, 1, "S")
+            widen(3, 1, 3, "S")
+            a_op(2, 3)
+            past_copy(2, 0, "S")
+            widen(3, 0, 2, "V")
+            past(2, 1)
+            widen(3, 0, 1, "V")
+            past_copy(2, 1, "S")
+            fut(2, 4)
+            ilv_z(3, 2, 0, "V")
             a_op(2, 4)
             fut(2, 5)
-            widen(3, 1, 3, "V")
-            widen(3, 1, 2, "V")
-            past(2, 0)
-            quant_past(1)
-            load_z(3, 1)
+            ilv_y(3, 0, 0, "S")
+            tr(4)
             fut(2, 6)
-            tr(9)
+            tr_copy(8, "S")
+            ilv_y(3, 0, 1, "V")
+            h_pass(1, 1)
             a_op(2, 5)
-            ilv_y(3, 0, 0, "V")
-            ilv_y(3, 0, 1, "S")
+            ilv_z(3, 1, 1, "S")
             fut(2, 7)
             ilv_y(3, 1, 0, "V")
-            past_copy(2, 0, "S")
-            past(2, 1)
-            ilv_z(3, 0, 0, "S")
-            ilv_y(3, 1, 1, "V")
-            h_pass(0, 1)
             tr_copy(9, "S")
-            past_copy(2, 1, "S")
-            quant_y(3, 0)
-            a_op(2, 6)
-            quant_y(3, 1)
-            a_op(2, 7)
-            h_pass(3, 1)
-            tr(10)
-            ilv_z(3, 0, 1, "V")
             past(2, 2)
-            fut(3, 0)
-            a_op(3, 0)
-            ilv_z(3, 1, 0, "S")
-            fut(3, 1)
-            tr_copy(10, "S")
-            h_pass(1, 1)
-            past_copy(2, 2, "S")
-            fut(3, 2)
-            ilv_z(3, 1, 1, "S")
-            load_z(3, 2)
-            tr(11)
-            ilv_z(3, 2, 0, "S")
-            a_op(3, 1)
-            fut(3, 3)
-            quant_z(3, 0)
+            a_op(2, 6)
+            ilv_y(3, 1, 1, "V")
+            quant_y(3, 0)
+            quant_y(3, 1)
             past(2, 3)
-            tr_copy(11, "S")
-            a_op(3, 2)
-            ilv_z(3, 2, 1, "V")
-            a_op(3, 3)
+            h_pass(3, 1)
+            a_op(2, 7)
+            ilv_z(3, 0, 1, "S")
+            past_copy(2, 3, "S")
+            fut(3, 0)
+            past_copy(2, 2, "S")
+            fut(3, 1)
+            ilv_z(3, 2, 1, "S")
+            tr(5)
+            quant_z(3, 0)
+            a_op(3, 0)
+            tr_copy(10, "S")
+            fut(3, 2)
+            a_op(3, 1)
             quant_z(3, 1)
             quant_z(3, 2)
-            quant_a(6, 2)
-            fut(3, 4)
-            past_copy(2, 3, "S")
-            fut(3, 5)
-            tr(12)
+            a_op(3, 2)
+            tr_copy(11, "S")
+            fut(3, 3)
+            a_op(3, 3)
             past(3, 0)
-            a_op(3, 4)
-            tr_copy(12, "S")
-            fut(3, 6)
-            past_copy(3, 0, "S")
-            a_op(3, 5)
-            tr(13)
-            tr_copy(13, "S")
-            a_op(3, 6)
-            quant_past(2)
             past(3, 1)
+            fut(3, 4)
+            past_copy(3, 0, "S")
+            quant_a(6, 2)
             quant_a(8, 2)
-            tr(14)
-            fut(3, 7)
+            fut(3, 5)
             past_copy(3, 1, "S")
+            tr(6)
+            tr_copy(12, "S")
+            a_op(3, 4)
+            a_op(3, 5)
+            fut(3, 6)
+            quant_past(2)
+            a_op(3, 6)
+            fut(3, 7)
+            tr_copy(13, "S")
             past(3, 2)
-            tr_copy(14, "V")
-            a_op(3, 7)
-            tr(15)
-            h_pass(4, 0)
-            past_copy(3, 2, "S")
             past(3, 3)
-            h_pass(0, 2)
-            past_copy(3, 3, "S")
-            tr_copy(15, "V")
-            quant_a(12, 2)
-            h_pass(6, 0)
-            h_pass(6, 1)
-            h_pass(7, 0)
-            h_pass(7, 1)
             quant_a(10, 2)
+            a_op(3, 7)
+            h_pass(3, 2)
+            h_pass(4, 0)
+            past_copy(3, 2, "V")
+            quant_a(12, 2)
             h_pass(1, 2)
+            h_pass(2, 2)
+            past_copy(3, 3, "S")
+            tr(7)
             quant_past(3)
-            quant_a(14, 2)
+            h_pass(0, 2)
             h_pass(0, 3)
+            tr_copy(15, "S")
+            h_pass(3, 3)
+            h_pass(4, 1)
+            h_pass(2, 3)
+            tr_copy(14, "S")
             h_pass(5, 0)
             h_out(0, "V")
+            h_pass(5, 1)
+            h_pass(4, 2)
+            h_out(2, "S")
+            quant_a(14, 2)
+            h_out(3, "V")
+            h_pass(4, 3)
             h_pass(1, 3)
-            h_pass(6, 2)
+            h_out(4, "V")
+            h_pass(5, 2)
+            h_pass(7, 0)
+            h_pass(5, 3)
+            h_pass(7, 1)
+            h_pass(7, 2)
             h_out(1, "V")
+            h_pass(7, 3)
+            h_pass(6, 0)
+            h_out(5, "V")
+            h_pass(6, 1)
+            h_pass(6, 2)
+            h_out(7, "S")
             h_pass(6, 3)
             h_out(6, "V")
-            h_pass(7, 2)
-            h_pass(7, 3)
-            h_pass(5, 1)
-            h_pass(5, 2)
-            h_pass(5, 3)
-            h_pass(4, 1)
-            h_pass(4, 2)
-            h_pass(4, 3)
-            h_out(7, "V")
-            h_pass(3, 2)
-            h_out(5, "S")
-            h_pass(3, 3)
-            h_out(4, "V")
-            h_pass(2, 1)
-            h_out(3, "S")
-            h_pass(2, 2)
-            h_pass(2, 3)
-            h_out(2, "V")

@@ -320,327 +320,327 @@ def tile_weighted_hankel_subspace_s11_kernel(
             nc.vector.tensor_copy(out=rhos[:], in_=rho16[:])
 
         with tc.manual_schedule():
-            load_y(0, 0)
-            clear_pws()
             small_loads()
-            load_y(0, 1)
-            load_y(1, 0)
-            widen(0, 0, 0, "V")
-            load_w(0, 2)
-            widen(0, 0, 1, "S")
+            load_y(0, 0)
+            widen(0, 0, 0, "S")
+            widen(0, 0, 1, "V")
             widen(0, 0, 3, "V")
-            widen(0, 0, 2, "V")
-            ilv_y(0, 0, 0, "V")
+            load_y(0, 1)
+            widen(0, 0, 2, "S")
+            load_y(1, 0)
+            load_w(0, 2)
             widen(0, 1, 0, "S")
-            load_z(0, 0)
             load_w(2, 2)
             widen(0, 1, 1, "S")
-            ilv_y(0, 0, 1, "V")
-            widen(0, 1, 2, "V")
-            load_w(4, 2)
-            load_w(6, 2)
-            widen(0, 1, 3, "S")
-            load_lam()
+            load_z(0, 0)
             w_transpose(1)
+            widen(0, 1, 3, "S")
+            load_w(4, 2)
             load_y(1, 1)
-            w_transpose(0)
-            quant_y(0, 0)
+            load_lam()
             load_z(0, 1)
-            widen(1, 0, 0, "S")
-            widen(1, 0, 2, "S")
-            widen(1, 0, 3, "S")
-            load_z(0, 2)
+            w_transpose(0)
             w_transpose(2)
-            load_pw()
-            ilv_y(0, 1, 0, "V")
+            load_w(6, 2)
+            clear_pws()
+            load_z(0, 2)
             w_transpose(3)
-            load_pws()
-            w_copy(0, "S")
+            widen(0, 1, 2, "V")
+            widen(1, 0, 0, "S")
+            widen(1, 0, 3, "S")
             load_y(2, 0)
-            load_z(1, 0)
-            load_z(1, 1)
-            ilv_y(0, 1, 1, "V")
-            widen(1, 0, 1, "S")
+            load_pw()
+            widen(1, 0, 1, "V")
+            widen(1, 0, 2, "S")
+            w_copy(0, "S")
+            ilv_y(0, 0, 0, "V")
+            ilv_y(0, 1, 0, "V")
             w_copy(1, "S")
-            ilv_y(1, 0, 0, "S")
-            w_copy(3, "S")
-            w_copy(2, "S")
-            load_z(1, 2)
-            widen_small()
-            ilv_z(0, 0, 0, "V")
-            ilv_z(0, 0, 1, "V")
-            quant_y(0, 1)
-            quant_z(0, 0)
             w_transpose(5)
-            w_transpose(4)
-            w_copy(4, "S")
-            w_quant(1, 0, 256)
-            load_y(2, 1)
-            w_copy(5, "S")
-            w_transpose(7)
-            w_transpose(6)
-            w_copy(7, "S")
-            w_quant(0, 0, 256)
-            load_z(2, 0)
-            fut(0, 0)
-            load_z(2, 1)
+            ilv_y(0, 1, 1, "V")
+            ilv_y(0, 0, 1, "V")
+            load_pws()
+            ilv_y(1, 0, 0, "V")
+            quant_y(0, 0)
+            load_z(1, 0)
             ilv_y(1, 0, 1, "V")
-            w_quant(0, 256, 256)
-            spread_lam(0)
+            ilv_z(0, 0, 0, "V")
+            quant_y(0, 1)
+            load_z(1, 1)
+            w_copy(2, "S")
             quant_y(1, 0)
-            w_copy(6, "S")
-            fut(0, 1)
-            w_quant(1, 256, 256)
-            w_quant(0, 512, 256)
-            w_quant(1, 512, 256)
-            widen(1, 1, 0, "V")
-            load_z(2, 2)
-            widen(1, 1, 1, "V")
-            w_quant(1, 768, 256)
+            w_copy(3, "S")
+            ilv_z(0, 0, 1, "S")
+            widen(1, 1, 0, "S")
+            w_quant(1, 0, 256)
+            w_copy(5, "S")
+            w_quant(0, 256, 256)
+            w_transpose(4)
+            widen(1, 1, 1, "S")
+            w_quant(0, 0, 256)
             widen(1, 1, 2, "S")
-            order_lam(0, 0, "S")
+            quant_z(0, 0)
+            widen_small()
             widen(1, 1, 3, "S")
-            w_quant(0, 768, 256)
-            a_op(0, 0)
+            w_quant(1, 256, 256)
             ilv_z(0, 1, 0, "V")
-            fut(0, 2)
-            ilv_z(0, 1, 1, "S")
-            a_op(0, 1)
-            a_op(0, 2)
-            ilv_z(0, 2, 0, "S")
+            w_copy(4, "S")
+            ilv_y(1, 1, 0, "V")
+            ilv_z(0, 1, 1, "V")
+            w_quant(1, 512, 256)
+            spread_lam(0)
+            order_lam(0, 0, "S")
+            w_quant(0, 512, 256)
             spread_lam(1)
-            fut(0, 3)
-            quant_z(0, 1)
-            ilv_z(0, 2, 1, "V")
-            a_op(0, 3)
-            fut(0, 4)
-            fut(0, 5)
-            a_op(0, 4)
-            load_y(3, 0)
-            fut(0, 6)
-            quant_z(0, 2)
-            ilv_y(1, 1, 0, "S")
-            a_op(0, 5)
             ilv_y(1, 1, 1, "S")
-            past(0, 0)
-            past(0, 1)
-            load_y(3, 1)
-            load_z(3, 0)
-            quant_y(1, 1)
-            order_lam(0, 1, "S")
-            order_lam(1, 0, "S")
-            load_z(3, 1)
-            a_op(0, 6)
             order_lam(1, 1, "S")
+            w_transpose(6)
+            w_copy(6, "S")
+            load_y(2, 1)
+            fut(0, 0)
+            w_transpose(7)
+            ilv_z(0, 2, 0, "V")
+            fut(0, 1)
+            load_z(1, 2)
+            a_op(0, 0)
+            a_op(0, 1)
+            load_z(2, 0)
+            fut(0, 2)
+            order_lam(1, 0, "S")
+            ilv_z(0, 2, 1, "S")
             widen(2, 0, 0, "S")
-            widen(2, 0, 3, "V")
-            fut(0, 7)
-            past_copy(0, 0, "S")
-            widen(2, 0, 1, "V")
-            past_copy(0, 1, "S")
-            tr(0)
-            widen(2, 0, 2, "V")
-            ilv_z(1, 0, 0, "S")
-            tr_copy(0, "S")
-            fut(1, 0)
-            ilv_y(2, 0, 0, "V")
-            past(0, 2)
-            tr_copy(1, "S")
-            past(0, 3)
+            load_y(3, 0)
+            widen(2, 0, 1, "S")
+            widen(2, 0, 2, "S")
+            order_lam(0, 1, "S")
+            quant_z(0, 1)
+            load_z(2, 1)
+            fut(0, 3)
+            load_z(2, 2)
+            a_op(0, 2)
+            a_op(0, 3)
+            quant_z(0, 2)
+            widen(2, 0, 3, "S")
+            quant_y(1, 1)
+            load_y(3, 1)
+            w_copy(7, "S")
+            ilv_y(2, 0, 0, "S")
             ilv_y(2, 0, 1, "V")
+            w_quant(0, 768, 256)
+            w_quant(1, 768, 256)
+            fut(0, 4)
+            a_op(0, 4)
+            fut(0, 5)
+            past(0, 0)
+            past_copy(0, 0, "S")
+            past(0, 1)
+            a_op(0, 5)
+            fut(0, 6)
+            past_copy(0, 1, "S")
+            ilv_z(1, 0, 0, "S")
+            tr(0)
+            fut(0, 7)
             ilv_z(1, 0, 1, "V")
-            ilv_z(1, 1, 0, "S")
+            tr_copy(0, "S")
+            a_op(0, 6)
+            tr_copy(1, "S")
+            ilv_z(1, 1, 0, "V")
+            fut(1, 0)
             quant_y(2, 0)
             a_op(0, 7)
-            fut(1, 1)
+            past(0, 2)
+            widen(2, 1, 0, "S")
             quant_z(1, 0)
-            past_copy(0, 2, "S")
-            ilv_z(1, 1, 1, "V")
-            past_copy(0, 3, "S")
+            past(0, 3)
             a_op(1, 0)
-            tr(1)
-            quant_z(1, 1)
-            fut(1, 2)
-            ilv_z(1, 2, 0, "V")
-            a_op(1, 1)
-            ilv_z(1, 2, 1, "S")
-            tr_copy(2, "S")
-            fut(1, 3)
-            tr_copy(3, "S")
-            widen(2, 1, 0, "V")
-            quant_z(1, 2)
-            load_z(3, 2)
-            ilv_z(2, 0, 0, "S")
-            a_op(1, 2)
-            past(1, 0)
-            quant_past(0)
-            ilv_z(2, 0, 1, "S")
-            a_op(1, 3)
+            ilv_z(1, 1, 1, "S")
             quant_a(0, 2)
-            past(1, 1)
-            fut(1, 4)
-            fut(1, 5)
-            past_copy(1, 0, "S")
-            widen(2, 1, 1, "V")
-            widen(2, 1, 2, "V")
-            h_pass(1, 0)
-            past_copy(1, 1, "S")
+            widen(2, 1, 2, "S")
+            fut(1, 1)
+            past_copy(0, 2, "S")
+            fut(1, 2)
+            load_z(3, 0)
+            ilv_z(1, 2, 0, "V")
+            past_copy(0, 3, "S")
+            ilv_z(2, 0, 0, "S")
+            ilv_z(1, 2, 1, "V")
+            a_op(1, 1)
+            tr(1)
+            tr_copy(2, "S")
+            widen(2, 1, 1, "S")
+            tr_copy(3, "S")
+            load_z(3, 1)
+            quant_z(1, 2)
+            a_op(1, 2)
+            fut(1, 3)
+            widen(2, 1, 3, "S")
             ilv_z(2, 1, 0, "S")
-            widen(2, 1, 3, "V")
+            quant_z(1, 1)
+            a_op(1, 3)
+            fut(1, 4)
+            past(1, 0)
+            past(1, 1)
+            past_copy(1, 0, "S")
+            past_copy(1, 1, "S")
+            fut(1, 5)
+            ilv_z(2, 0, 1, "V")
+            load_z(3, 2)
+            quant_past(0)
             a_op(1, 4)
+            ilv_z(2, 1, 1, "V")
+            ilv_y(2, 1, 0, "V")
             a_op(1, 5)
+            ilv_z(2, 2, 0, "S")
+            fut(1, 6)
             tr(2)
             tr_copy(4, "S")
-            ilv_y(2, 1, 0, "V")
-            fut(1, 6)
-            quant_z(2, 0)
             ilv_y(2, 1, 1, "V")
-            ilv_z(2, 2, 0, "S")
-            a_op(1, 6)
             tr_copy(5, "S")
             fut(1, 7)
-            h_pass(3, 0)
-            widen(3, 0, 0, "S")
-            past(1, 2)
+            a_op(1, 6)
             quant_y(2, 1)
-            past_copy(1, 2, "S")
-            widen(3, 1, 0, "V")
-            h_pass(0, 0)
-            fut(2, 0)
             a_op(1, 7)
-            widen(3, 1, 2, "V")
-            ilv_z(2, 2, 1, "V")
-            quant_a(4, 2)
+            past(1, 2)
+            fut(2, 0)
+            h_pass(1, 0)
             past(1, 3)
-            ilv_z(2, 1, 1, "S")
-            h_pass(2, 0)
-            a_op(2, 0)
+            widen(3, 0, 0, "S")
+            widen(3, 1, 0, "S")
+            quant_z(2, 0)
+            widen(3, 0, 3, "S")
             fut(2, 1)
-            past_copy(1, 3, "S")
-            quant_z(2, 2)
-            a_op(2, 1)
-            tr(3)
-            ilv_z(3, 0, 0, "S")
-            quant_past(1)
-            quant_z(2, 1)
+            a_op(2, 0)
             fut(2, 2)
-            fut(2, 3)
-            tr_copy(6, "S")
-            h_pass(2, 1)
-            ilv_z(3, 1, 0, "S")
-            a_op(2, 2)
-            quant_a(2, 2)
-            h_pass(0, 1)
-            past(2, 0)
-            widen(3, 0, 3, "V")
-            tr_copy(7, "S")
             widen(3, 1, 1, "S")
-            widen(3, 1, 3, "S")
+            past_copy(1, 2, "S")
+            past_copy(1, 3, "S")
+            widen(3, 1, 2, "S")
+            widen(3, 0, 2, "S")
+            widen(3, 0, 1, "S")
+            tr(3)
+            ilv_z(2, 2, 1, "V")
+            ilv_z(3, 0, 0, "V")
+            tr_copy(6, "S")
+            a_op(2, 1)
+            h_pass(0, 0)
+            quant_z(2, 2)
+            a_op(2, 2)
+            quant_z(2, 1)
+            fut(2, 3)
+            h_pass(3, 0)
+            quant_a(4, 2)
+            tr_copy(7, "S")
+            quant_a(2, 2)
             a_op(2, 3)
-            past_copy(2, 0, "S")
-            widen(3, 0, 2, "V")
-            past(2, 1)
-            widen(3, 0, 1, "V")
-            past_copy(2, 1, "S")
             fut(2, 4)
-            ilv_z(3, 2, 0, "V")
             a_op(2, 4)
+            past(2, 0)
+            past(2, 1)
             fut(2, 5)
+            widen(3, 1, 3, "S")
             ilv_y(3, 0, 0, "S")
-            tr(4)
+            past_copy(2, 0, "S")
             fut(2, 6)
-            tr_copy(8, "S")
-            ilv_y(3, 0, 1, "V")
-            h_pass(1, 1)
-            a_op(2, 5)
-            ilv_z(3, 1, 1, "S")
-            fut(2, 7)
+            quant_past(1)
             ilv_y(3, 1, 0, "V")
-            tr_copy(9, "S")
-            past(2, 2)
+            past_copy(2, 1, "S")
+            tr(4)
+            a_op(2, 5)
+            fut(2, 7)
+            ilv_z(3, 1, 0, "S")
+            h_pass(1, 1)
+            ilv_y(3, 0, 1, "V")
+            tr_copy(8, "S")
+            ilv_y(3, 1, 1, "S")
             a_op(2, 6)
-            ilv_y(3, 1, 1, "V")
-            quant_y(3, 0)
-            quant_y(3, 1)
-            past(2, 3)
-            h_pass(3, 1)
-            a_op(2, 7)
+            past(2, 2)
+            h_pass(2, 0)
+            h_pass(0, 1)
+            tr_copy(9, "S")
             ilv_z(3, 0, 1, "S")
-            past_copy(2, 3, "S")
+            ilv_z(3, 2, 0, "V")
+            a_op(2, 7)
+            quant_y(3, 0)
+            h_pass(3, 1)
+            quant_y(3, 1)
+            ilv_z(3, 1, 1, "V")
+            quant_z(3, 0)
+            past(2, 3)
             fut(3, 0)
             past_copy(2, 2, "S")
             fut(3, 1)
+            h_pass(2, 1)
+            past_copy(2, 3, "S")
             ilv_z(3, 2, 1, "S")
-            tr(5)
-            quant_z(3, 0)
             a_op(3, 0)
+            tr(5)
             tr_copy(10, "S")
-            fut(3, 2)
             a_op(3, 1)
+            fut(3, 2)
             quant_z(3, 1)
-            quant_z(3, 2)
-            a_op(3, 2)
-            tr_copy(11, "S")
             fut(3, 3)
-            a_op(3, 3)
+            quant_z(3, 2)
+            tr_copy(11, "S")
             past(3, 0)
             past(3, 1)
-            fut(3, 4)
+            quant_past(2)
+            a_op(3, 2)
             past_copy(3, 0, "S")
+            a_op(3, 3)
+            quant_a(10, 2)
             quant_a(6, 2)
-            quant_a(8, 2)
+            fut(3, 4)
             fut(3, 5)
+            a_op(3, 4)
+            quant_a(8, 2)
+            a_op(3, 5)
             past_copy(3, 1, "S")
             tr(6)
-            tr_copy(12, "S")
-            a_op(3, 4)
-            a_op(3, 5)
             fut(3, 6)
-            quant_past(2)
-            a_op(3, 6)
-            fut(3, 7)
-            tr_copy(13, "S")
-            past(3, 2)
-            past(3, 3)
-            quant_a(10, 2)
-            a_op(3, 7)
+            tr_copy(12, "V")
             h_pass(3, 2)
-            h_pass(4, 0)
-            past_copy(3, 2, "V")
+            tr_copy(13, "S")
+            fut(3, 7)
             quant_a(12, 2)
+            past(3, 2)
+            a_op(3, 6)
+            past(3, 3)
+            h_pass(0, 2)
             h_pass(1, 2)
             h_pass(2, 2)
+            a_op(3, 7)
             past_copy(3, 3, "S")
+            past_copy(3, 2, "V")
+            h_pass(4, 0)
             tr(7)
-            quant_past(3)
-            h_pass(0, 2)
-            h_pass(0, 3)
-            tr_copy(15, "S")
-            h_pass(3, 3)
             h_pass(4, 1)
-            h_pass(2, 3)
             tr_copy(14, "S")
-            h_pass(5, 0)
-            h_out(0, "V")
-            h_pass(5, 1)
-            h_pass(4, 2)
+            quant_past(3)
+            tr_copy(15, "V")
+            h_pass(0, 3)
+            h_out(0, "S")
+            h_pass(2, 3)
             h_out(2, "S")
-            quant_a(14, 2)
-            h_out(3, "V")
-            h_pass(4, 3)
             h_pass(1, 3)
-            h_out(4, "V")
-            h_pass(5, 2)
-            h_pass(7, 0)
-            h_pass(5, 3)
-            h_pass(7, 1)
-            h_pass(7, 2)
-            h_out(1, "V")
-            h_pass(7, 3)
             h_pass(6, 0)
-            h_out(5, "V")
+            h_pass(3, 3)
+            quant_a(14, 2)
+            h_pass(4, 2)
             h_pass(6, 1)
             h_pass(6, 2)
-            h_out(7, "S")
+            h_pass(4, 3)
+            h_pass(5, 0)
+            h_pass(5, 1)
+            h_out(1, "V")
+            h_pass(5, 2)
+            h_pass(5, 3)
             h_pass(6, 3)
+            h_out(3, "V")
+            h_out(4, "V")
+            h_out(5, "S")
+            h_pass(7, 0)
+            h_pass(7, 1)
+            h_pass(7, 2)
+            h_pass(7, 3)
             h_out(6, "V")
+            h_out(7, "V")

from contextlib import ExitStack

import concourse.mybir as mybir
from concourse.masks import make_identity

R, F, T, D, C = 1024, 1024, 2048, 1536, 512
FLOPS = 2 * (R * F * T + T * D * C + R * T * C)

F32 = mybir.dt.float32
BF16 = mybir.dt.bfloat16
U32 = mybir.dt.uint32
I32 = mybir.dt.int32
U8 = mybir.dt.uint8
FP8 = mybir.dt.float8_e4m3fn
FP8X4 = mybir.dt.float8_e4m3fn_x4
FP4X4 = mybir.dt.float4_e2m1fn_x4
ADD = mybir.AluOpType.add
MULT = mybir.AluOpType.mult
COPY = mybir.ActivationFunctionType.Copy

P = 128
GROUPS = T // 512
FP = F // 512
DP = D // 512
RT = R // P
OPEN = 4


def tile_weighted_hankel_subspace_s11_kernel(
    tc, w_f, y_f_bytes, y_f_scale, z_p, w_p_words, w_p_scales, level, lam, rho, out
):
    nc = tc.nc
    with ExitStack() as ctx:
        keep = ctx.enter_context(tc.tile_pool(name="keep", bufs=1))
        work = ctx.enter_context(tc.tile_pool(name="work", bufs=2))
        psum = ctx.enter_context(tc.psum_pool(name="psum", bufs=1))

        ident = keep.tile([P, P], F32, name="ident")

        make_identity(nc, ident[:])
        y_scale = keep.tile([P, FP, 4], F32, name="y_scale")
        lev16 = keep.tile([P, RT], BF16, name="lev16")
        rho16 = keep.tile([P, RT], BF16, name="rho16")
        lev = keep.tile([P, RT], F32, name="lev")
        rhos = keep.tile([P, RT], F32, name="rhos")
        lam_row = keep.tile([P, T], BF16, name="lam_row")
        ones = keep.tile([P, P], BF16, name="ones")
        nc.gpsimd.memset(lam_row[:], 0.0)
        nc.gpsimd.memset(ones[:], 1.0)
        lam_ord = keep.tile([P, T], BF16, name="lam_ord")
        wf = keep.tile([P, RT, F], BF16, name="wf", align_bytes=64)
        wi = keep.tile([P, FP, R, 4], BF16, name="wi", align_bytes=64)
        wcode = keep.tile([P, FP, R], U32, name="wcode", align_bytes=64)
        wscale = keep.tile([P, FP, R], U8, name="wscale", align_bytes=64)
        pw = keep.tile([P, DP, 2 * C], U8, name="pw", align_bytes=64)
        pws = keep.tile([P, DP, C], U8, name="pws", align_bytes=64)
        acode = keep.tile([P, GROUPS, R], U32, name="acode", align_bytes=64)
        ascale = keep.tile([P, GROUPS, R], U8, name="ascale", align_bytes=64)
        bcode = keep.tile([P, GROUPS, C], U32, name="bcode", align_bytes=64)
        bscale = keep.tile([P, GROUPS, C], U8, name="bscale", align_bytes=64)

        y_view = y_f_bytes.rearrange("(g p t) n -> g p t n", g=FP, p=P, t=4)
        z_view = z_p.rearrange("(g p t) n -> g p t n", g=DP, p=P, t=4)
        w_view = w_f.rearrange("(p c) f -> p c f", c=RT)
        out_view = out.rearrange("(p c) n -> p c n", c=RT)

        tiles = {}

        def load_y(g, f):
            if f == 0:
                tiles["yb", g] = work.tile([P, FP, 4, 512], U8, name="yb", align_bytes=64)
            step = 2 if (g, f) == (0, 0) else 4
            for t in range(0, 4, step):
                nc.sync.dma_start(
                    out=tiles["yb", g][:, f, t : t + step, :], in_=y_view[f][:, t : t + step, 512 * g : 512 * g + 512]
                )

        def load_z(g, d):
            zr = work.tile([P, 4, 512], BF16, name="zr", bufs=8, align_bytes=64)
            nc.sync.dma_start(out=zr[:], in_=z_view[d][:, :, 512 * g : 512 * g + 512])
            tiles["zr", g, d] = zr

        def load_w(c0, n):
            nc.sync.dma_start(out=wf[:, c0 : c0 + n, :], in_=w_view[:, c0 : c0 + n, :])

        def widen(g, f, t, eng):
            if t == 0:
                tiles["yw", g, f] = work.tile([P, 4, 512], BF16, name="yw", bufs=3, align_bytes=64)
            src = tiles["yb", g][:, f, t, :].bitcast(FP8)
            dst = tiles["yw", g, f][:, t, :]
            s = y_scale[:, f, t : t + 1]
            if eng == "S":
                nc.scalar.activation(out=dst, in_=src, func=COPY, scale=s)
            else:
                nc.vector.tensor_scalar(out=dst, in0=src, scalar1=s, scalar2=None, op0=MULT)

        def ilv_y(g, f, u, eng):
            if u == 0:
                tiles["yi", g, f] = work.tile([P, 512, 4], BF16, name="yi", bufs=3, align_bytes=64)
            dst = tiles["yi", g, f][:, 256 * u : 256 * u + 256, :].rearrange("p (q e) t -> p q t e", e=2)
            src = tiles["yw", g, f][:].rearrange("p t (q u e) -> p u q t e", u=2, e=2)[:, u]
            if eng == "S":
                nc.scalar.copy(out=dst, in_=src)
            else:
                nc.vector.tensor_copy(out=dst, in_=src)

        def quant_y(g, f):
            if f == 0:
                tiles["yc", g] = work.tile([P, FP, 512], U32, name="yc", align_bytes=64)
                tiles["ys", g] = work.tile([P, FP, 512], U8, name="ys", align_bytes=64)
            nc.vector.quantize_mx(
                out=tiles["yc", g][:, f, :].bitcast(FP8X4),
                scales=tiles["ys", g][:, f, :],
                in_=tiles["yi", g, f][:].rearrange("p n t -> p (n t)"),
            )

        def ilv_z(g, d, h, eng):
            if h == 0:
                tiles["zi", g, d] = work.tile([P, 4, 128, 4], BF16, name="zi", bufs=4, align_bytes=64)
            dst = tiles["zi", g, d][:].rearrange("p s m j -> p m j s")[:, 64 * h : 64 * h + 64]
            src = tiles["zr", g, d][:].rearrange("p j (m s) -> p m j s", s=4)[:, 64 * h : 64 * h + 64]
            if eng == "S":
                nc.scalar.copy(out=dst, in_=src)
            else:
                nc.vector.tensor_copy(out=dst, in_=src)

        def quant_z(g, d):
            if d == 0:
                tiles["zc", g] = work.tile([P, DP, 512], U32, name="zc", align_bytes=64)
                tiles["zs", g] = work.tile([P, DP, 512], U8, name="zs", align_bytes=64)
            nc.vector.quantize_mx(
                out=tiles["zc", g][:, d, :].bitcast(FP8X4),
                scales=tiles["zs", g][:, d, :],
                in_=tiles["zi", g, d][:].rearrange("p s m j -> p (s m j)"),
            )

        def w_transpose(c):
            tag = W_TAGS[c]
            wt = psum.tile([P, FP, 2, P], F32, name=tag, bufs=PS[tag])
            words = wf[:, c, :].bitcast(F32)
            for f in range(FP):
                for u in range(2):
                    nc.tensor.transpose(wt[:, f, u, :], words[:, 256 * f + u : 256 * (f + 1) : 2], ident[:])
            tiles["wt", c] = wt

        def w_copy(c, eng):
            dst = wi[:].rearrange("p f r j -> p (f r j)").bitcast(F32)
            dst = dst.rearrange("p (f r u) -> p f r u", f=FP, u=2)[:, :, P * c : P * c + P, :]
            src = tiles["wt", c][:].rearrange("p f u r -> p f r u")
            if eng == "S":
                nc.scalar.copy(out=dst, in_=src)
            else:
                nc.vector.tensor_copy(out=dst, in_=src)

        def w_quant(f, r0, n):
            nc.vector.quantize_mx(
                out=wcode[:, f, r0 : r0 + n].bitcast(FP8X4),
                scales=wscale[:, f, r0 : r0 + n],
                in_=wi[:, f, r0 : r0 + n, :].rearrange("p r j -> p (r j)"),
            )

        PS = {"fut": 2, "past": 2}
        W_TAGS = ["fut", "past", "fut", "past", "fut", "past", "fut", "past"]
        H_TAGS = ["h0", "h1", "h2", "h3", "fut", "past", "fut", "past"]

        def past(g, cc):
            pp = psum.tile([P, 4, 128], F32, name="past", bufs=PS["past"])
            for s in range(4):
                for d in range(DP):
                    nc.tensor.matmul_mx(
                        out=pp[:, s, :],
                        lhsT=tiles["zc", g][:, d, 128 * s : 128 * s + 128].bitcast(FP8X4),
                        lhsT_scale=tiles["zs", g][:, d, 128 * s : 128 * s + 128],
                        rhs=pw[:, d, 256 * cc : 256 * cc + 256].bitcast(FP4X4),
                        rhs_scale=pws[:, d, 128 * cc : 128 * cc + 128],
                        start=(d == 0),
                        stop=(d == DP - 1),
                    )
            tiles["pp", g, cc] = pp

        def past_copy(g, cc, eng):
            if cc == 0:
                tiles["pi", g] = work.tile([P, 512, 4], BF16, name="pi", align_bytes=64)
            dst = tiles["pi", g][:, 128 * cc : 128 * cc + 128, :]
            src = tiles["pp", g, cc][:].rearrange("p s n -> p n s")
            if eng == "S":
                nc.scalar.copy(out=dst, in_=src)
            else:
                nc.vector.tensor_copy(out=dst, in_=src)

        def quant_past(g):
            nc.vector.quantize_mx(
                out=bcode[:, g, :].bitcast(FP8X4),
                scales=bscale[:, g, :],
                in_=tiles["pi", g][:].rearrange("p n s -> p (n s)"),
            )

        def fut(g, c):
            fp = psum.tile([P, 512], F32, name="fut", bufs=PS["fut"])
            for f in range(FP):
                nc.tensor.matmul_mx(
                    out=fp[:],
                    lhsT=wcode[:, f, P * c : P * c + P].bitcast(FP8X4),
                    lhsT_scale=wscale[:, f, P * c : P * c + P],
                    rhs=tiles["yc", g][:, f, :].bitcast(FP8X4),
                    rhs_scale=tiles["ys", g][:, f, :],
                    start=(f == 0),
                    stop=(f == FP - 1),
                )
            tiles["fp", g, c] = fp

        def a_op(g, c):
            at = work.tile([P, 512], BF16, name="at", bufs=7, align_bytes=64)
            nc.vector.scalar_tensor_tensor(
                out=at[:],
                in0=tiles["fp", g, c][:],
                scalar=lev[:, c : c + 1],
                in1=lam_ord[:, 512 * g : 512 * g + 512],
                op0=ADD,
                op1=MULT,
            )
            tiles["at", g, c] = at

        def tr(q):
            for k in range(2):
                tp = psum.tile([P, 2, 2, P], F32, name="past", bufs=PS["past"])
                for i in range(2):
                    j = 4 * q + 2 * k + i
                    words = tiles["at", j // RT, j % RT][:].bitcast(F32)
                    for u in range(2):
                        nc.tensor.transpose(tp[:, i, u, :], words[:, P * u : P * u + P], ident[:])
                tiles["tp", 2 * q + k] = tp

        def tr_copy(q, eng):
            g, c0 = q // 4, 2 * (q % 4)
            if c0 == 0:
                tiles["ai", g] = work.tile([P, R, 4], BF16, name="ai", align_bytes=64)
            dst = tiles["ai", g][:].rearrange("p r j -> p (r j)").bitcast(F32)
            dst = dst.rearrange("p (c r u) -> p c r u", r=P, u=2)[:, c0 : c0 + 2]
            src = tiles["tp", q][:].rearrange("p c u r -> p c r u")
            if eng == "S":
                nc.scalar.copy(out=dst, in_=src)
            else:
                nc.vector.tensor_copy(out=dst, in_=src)

        def quant_a(q, n):
            g, r0 = q // 4, 256 * (q % 4)
            nc.vector.quantize_mx(
                out=acode[:, g, r0 : r0 + 256 * n].bitcast(FP8X4),
                scales=ascale[:, g, r0 : r0 + 256 * n],
                in_=tiles["ai", g][:, r0 : r0 + 256 * n, :].rearrange("p r j -> p (r j)"),
            )

        def h_pass(c, g):
            tag = H_TAGS[c]
            if g == 0:
                tiles["h", c] = psum.tile([P, C], F32, name=tag, bufs=PS.get(tag, 1))
            nc.tensor.matmul_mx(
                out=tiles["h", c][:],
                lhsT=acode[:, g, P * c : P * c + P].bitcast(FP8X4),
                lhsT_scale=ascale[:, g, P * c : P * c + P],
                rhs=bcode[:, g, :].bitcast(FP8X4),
                rhs_scale=bscale[:, g, :],
                start=(g == 0),
                stop=(g == GROUPS - 1),
            )

        def h_out(c, eng):
            if c == 0:
                tiles["ho"] = keep.tile([P, RT, C], F32, name="wf", align_bytes=64)
            ho = tiles["ho"][:, c, :]
            if eng == "S":
                nc.scalar.activation(out=ho, in_=tiles["h", c][:], func=COPY, scale=rhos[:, c : c + 1])
            else:
                nc.vector.tensor_scalar(
                    out=ho, in0=tiles["h", c][:], scalar1=rhos[:, c : c + 1], scalar2=None, op0=MULT
                )
            nc.sync.dma_start(out=out_view[:, c, :], in_=ho)

        def load_lam():
            nc.sync.dma_start(out=lam_row[0:1, :], in_=lam.rearrange("(o n) -> o n", o=1))

        def spread_lam(i):
            lp = psum.tile([P, 2, 512], BF16, name="h%d" % i)
            for k in range(2):
                g = 2 * i + k
                nc.tensor.matmul(out=lp[:, k, :], lhsT=ones[:], rhs=lam_row[:, 512 * g : 512 * g + 512], start=True, stop=True)
            tiles["lp", i] = lp

        def order_lam(i, k, eng):
            g = 2 * i + k
            dst = lam_ord[:, 512 * g : 512 * g + 512].rearrange("p (u q e) -> p u q e", u=2, e=2)
            src = tiles["lp", i][:, k, :].rearrange("p (q u e) -> p u q e", u=2, e=2)
            if eng == "S":
                nc.scalar.copy(out=dst, in_=src)
            else:
                nc.vector.tensor_copy(out=dst, in_=src)


        def small_loads():
            nc.scalar.dma_start(out=y_scale[:], in_=y_f_scale.rearrange("(g p t) o -> p g (t o)", g=FP, p=P, t=4))
            nc.scalar.dma_start(out=lev16[:], in_=level.rearrange("(p c) -> p c", c=RT))
            nc.scalar.dma_start(out=rho16[:], in_=rho.rearrange("(p c) -> p c", c=RT))

        def load_pw():
            nc.sync.dma_start(out=pw[:], in_=w_p_words.rearrange("d p n -> p d n"))

        def clear_pws():
            nc.vector.memset(pws[:].rearrange("p d n -> p (d n)").bitcast(I32), 0)

        def load_pws():
            for q in range(4):
                nc.sync.dma_start(
                    out=pws[32 * q : 32 * q + 4, :, :].bitcast(I32),
                    in_=w_p_scales[:, 4 * q : 4 * q + 4, :].rearrange("d q n -> q d n").bitcast(I32),
                )

        def widen_small():
            nc.vector.tensor_copy(out=lev[:], in_=lev16[:])
            nc.vector.tensor_copy(out=rhos[:], in_=rho16[:])

        with tc.manual_schedule():
            small_loads()
            load_y(0, 0)
            widen(0, 0, 0, "S")
            widen(0, 0, 1, "V")
            widen(0, 0, 3, "V")
            load_y(0, 1)
            widen(0, 0, 2, "S")
            load_y(1, 0)
            load_w(0, 2)
            widen(0, 1, 0, "S")
            load_w(2, 2)
            widen(0, 1, 1, "S")
            load_z(0, 0)
            w_transpose(1)
            widen(0, 1, 3, "S")
            load_w(4, 2)
            load_y(1, 1)
            load_lam()
            load_z(0, 1)
            w_transpose(0)
            w_transpose(2)
            load_w(6, 2)
            clear_pws()
            load_z(0, 2)
            w_transpose(3)
            widen(0, 1, 2, "V")
            widen(1, 0, 0, "S")
            widen(1, 0, 3, "S")
            load_y(2, 0)
            load_pw()
            widen(1, 0, 1, "V")
            widen(1, 0, 2, "S")
            w_copy(0, "S")
            ilv_y(0, 0, 0, "V")
            ilv_y(0, 1, 0, "V")
            w_copy(1, "S")
            w_transpose(5)
            ilv_y(0, 1, 1, "V")
            ilv_y(0, 0, 1, "V")
            load_pws()
            ilv_y(1, 0, 0, "V")
            quant_y(0, 0)
            load_z(1, 0)
            ilv_y(1, 0, 1, "V")
            ilv_z(0, 0, 0, "V")
            quant_y(0, 1)
            load_z(1, 1)
            w_copy(2, "S")
            quant_y(1, 0)
            w_copy(3, "S")
            ilv_z(0, 0, 1, "S")
            widen(1, 1, 0, "S")
            w_quant(1, 0, 256)
            w_copy(5, "S")
            w_quant(0, 256, 256)
            w_transpose(4)
            widen(1, 1, 1, "S")
            w_quant(0, 0, 256)
            widen(1, 1, 2, "S")
            quant_z(0, 0)
            widen_small()
            widen(1, 1, 3, "S")
            w_quant(1, 256, 256)
            ilv_z(0, 1, 0, "V")
            w_copy(4, "S")
            ilv_y(1, 1, 0, "V")
            ilv_z(0, 1, 1, "V")
            w_quant(1, 512, 256)
            spread_lam(0)
            order_lam(0, 0, "S")
            w_quant(0, 512, 256)
            spread_lam(1)
            ilv_y(1, 1, 1, "S")
            order_lam(1, 1, "S")
            w_transpose(6)
            w_copy(6, "S")
            load_y(2, 1)
            fut(0, 0)
            w_transpose(7)
            ilv_z(0, 2, 0, "V")
            fut(0, 1)
            load_z(1, 2)
            a_op(0, 0)
            a_op(0, 1)
            load_z(2, 0)
            fut(0, 2)
            order_lam(1, 0, "S")
            ilv_z(0, 2, 1, "S")
            widen(2, 0, 0, "S")
            load_y(3, 0)
            widen(2, 0, 1, "S")
            widen(2, 0, 2, "S")
            order_lam(0, 1, "S")
            quant_z(0, 1)
            load_z(2, 1)
            fut(0, 3)
            load_z(2, 2)
            a_op(0, 2)
            a_op(0, 3)
            quant_z(0, 2)
            widen(2, 0, 3, "S")
            quant_y(1, 1)
            load_y(3, 1)
            w_copy(7, "S")
            ilv_y(2, 0, 0, "S")
            ilv_y(2, 0, 1, "V")
            w_quant(0, 768, 256)
            w_quant(1, 768, 256)
            fut(0, 4)
            a_op(0, 4)
            fut(0, 5)
            past(0, 0)
            past_copy(0, 0, "S")
            past(0, 1)
            a_op(0, 5)
            fut(0, 6)
            past_copy(0, 1, "S")
            ilv_z(1, 0, 0, "S")
            tr(0)
            fut(0, 7)
            ilv_z(1, 0, 1, "V")
            tr_copy(0, "S")
            a_op(0, 6)
            tr_copy(1, "S")
            ilv_z(1, 1, 0, "V")
            fut(1, 0)
            quant_y(2, 0)
            a_op(0, 7)
            past(0, 2)
            widen(2, 1, 0, "S")
            quant_z(1, 0)
            past(0, 3)
            a_op(1, 0)
            ilv_z(1, 1, 1, "S")
            quant_a(0, 2)
            widen(2, 1, 2, "S")
            fut(1, 1)
            past_copy(0, 2, "S")
            fut(1, 2)
            load_z(3, 0)
            ilv_z(1, 2, 0, "V")
            past_copy(0, 3, "S")
            ilv_z(2, 0, 0, "S")
            ilv_z(1, 2, 1, "V")
            a_op(1, 1)
            tr(1)
            tr_copy(2, "S")
            widen(2, 1, 1, "S")
            tr_copy(3, "S")
            load_z(3, 1)
            quant_z(1, 2)
            a_op(1, 2)
            fut(1, 3)
            widen(2, 1, 3, "S")
            ilv_z(2, 1, 0, "S")
            quant_z(1, 1)
            a_op(1, 3)
            fut(1, 4)
            past(1, 0)
            past(1, 1)
            past_copy(1, 0, "S")
            past_copy(1, 1, "S")
            fut(1, 5)
            ilv_z(2, 0, 1, "V")
            load_z(3, 2)
            quant_past(0)
            a_op(1, 4)
            ilv_z(2, 1, 1, "V")
            ilv_y(2, 1, 0, "V")
            a_op(1, 5)
            ilv_z(2, 2, 0, "S")
            fut(1, 6)
            tr(2)
            tr_copy(4, "S")
            ilv_y(2, 1, 1, "V")
            tr_copy(5, "S")
            fut(1, 7)
            a_op(1, 6)
            quant_y(2, 1)
            a_op(1, 7)
            past(1, 2)
            fut(2, 0)
            h_pass(1, 0)
            past(1, 3)
            widen(3, 0, 0, "S")
            widen(3, 1, 0, "S")
            quant_z(2, 0)
            widen(3, 0, 3, "S")
            fut(2, 1)
            a_op(2, 0)
            fut(2, 2)
            widen(3, 1, 1, "S")
            past_copy(1, 2, "S")
            past_copy(1, 3, "S")
            widen(3, 1, 2, "S")
            widen(3, 0, 2, "S")
            widen(3, 0, 1, "S")
            tr(3)
            ilv_z(2, 2, 1, "V")
            ilv_z(3, 0, 0, "V")
            tr_copy(6, "S")
            a_op(2, 1)
            h_pass(0, 0)
            quant_z(2, 2)
            a_op(2, 2)
            quant_z(2, 1)
            fut(2, 3)
            h_pass(3, 0)
            quant_a(4, 2)
            tr_copy(7, "S")
            quant_a(2, 2)
            a_op(2, 3)
            fut(2, 4)
            a_op(2, 4)
            past(2, 0)
            past(2, 1)
            fut(2, 5)
            widen(3, 1, 3, "S")
            ilv_y(3, 0, 0, "S")
            past_copy(2, 0, "S")
            fut(2, 6)
            quant_past(1)
            ilv_y(3, 1, 0, "V")
            past_copy(2, 1, "S")
            tr(4)
            a_op(2, 5)
            fut(2, 7)
            ilv_z(3, 1, 0, "S")
            h_pass(1, 1)
            ilv_y(3, 0, 1, "V")
            tr_copy(8, "S")
            ilv_y(3, 1, 1, "S")
            a_op(2, 6)
            past(2, 2)
            h_pass(2, 0)
            h_pass(0, 1)
            tr_copy(9, "S")
            ilv_z(3, 0, 1, "S")
            ilv_z(3, 2, 0, "V")
            a_op(2, 7)
            quant_y(3, 0)
            h_pass(3, 1)
            quant_y(3, 1)
            ilv_z(3, 1, 1, "V")
            quant_z(3, 0)
            past(2, 3)
            fut(3, 0)
            past_copy(2, 2, "S")
            fut(3, 1)
            h_pass(2, 1)
            past_copy(2, 3, "S")
            ilv_z(3, 2, 1, "S")
            a_op(3, 0)
            tr(5)
            tr_copy(10, "S")
            a_op(3, 1)
            fut(3, 2)
            quant_z(3, 1)
            fut(3, 3)
            quant_z(3, 2)
            tr_copy(11, "S")
            past(3, 0)
            past(3, 1)
            quant_past(2)
            a_op(3, 2)
            past_copy(3, 0, "S")
            a_op(3, 3)
            quant_a(10, 2)
            quant_a(6, 2)
            fut(3, 4)
            fut(3, 5)
            a_op(3, 4)
            quant_a(8, 2)
            a_op(3, 5)
            past_copy(3, 1, "S")
            tr(6)
            fut(3, 6)
            tr_copy(12, "V")
            h_pass(3, 2)
            tr_copy(13, "S")
            fut(3, 7)
            quant_a(12, 2)
            past(3, 2)
            a_op(3, 6)
            past(3, 3)
            h_pass(0, 2)
            h_pass(1, 2)
            h_pass(2, 2)
            a_op(3, 7)
            past_copy(3, 3, "S")
            past_copy(3, 2, "V")
            h_pass(4, 0)
            tr(7)
            h_pass(4, 1)
            tr_copy(14, "S")
            quant_past(3)
            tr_copy(15, "V")
            h_pass(0, 3)
            h_out(0, "S")
            h_pass(2, 3)
            h_out(2, "S")
            h_pass(1, 3)
            h_pass(6, 0)
            h_pass(3, 3)
            quant_a(14, 2)
            h_pass(4, 2)
            h_pass(6, 1)
            h_pass(6, 2)
            h_pass(4, 3)
            h_pass(5, 0)
            h_pass(5, 1)
            h_out(1, "V")
            h_pass(5, 2)
            h_pass(5, 3)
            h_pass(6, 3)
            h_out(3, "V")
            h_out(4, "V")
            h_out(5, "S")
            h_pass(7, 0)
            h_pass(7, 1)
            h_pass(7, 2)
            h_pass(7, 3)
            h_out(6, "V")
            h_out(7, "V")
